import numpy as np, ml_dtypes
CORES = [9,25,41,57]
N = 4
BF = ml_dtypes.bfloat16
def gentries(a):
    return np.ascontiguousarray(a.reshape(8, 16, -1).transpose(0, 2, 1)).reshape(8, -1)
def gtable(e):
    e = np.asarray(e); return np.ascontiguousarray(e.reshape(8, -1, 16).transpose(0, 2, 1)).reshape(128, -1).astype(np.int32)
M, L, S, ST = 512, 5, 512, 10
LPR, C, W = 4, 2628, 10528
LEV = [(16, LPR, 0), (32, 16 * LPR, LPR)] + [(288 + d * N * M, M, 17 * LPR + d * M) for d in range(L)]
START = np.array([v[0] for v in LEV]); SIZE = np.array([v[1] for v in LEV])
A8 = np.arange(8)[:, None]
def grow(rng, bias):
    tri = np.zeros((N, 8, 16, C), np.int64); par = np.zeros((N, 8, C - LPR), np.int64); let = np.zeros((N, 8, C - LPR), np.int64)
    G = np.zeros((8, 16, W), np.int64); G[:, :, 0] = 16 + np.arange(16)
    D = [np.repeat(G[:, :, :1], LPR, axis=2) for r in range(N)]
    for d in range(len(LEV)):
        b, m, o = LEV[d]; new = []
        for r in range(N):
            own = tri[r, :, :, o:o + m]
            if d + 1 < len(LEV):
                b2, m2, o2 = LEV[d + 1]
                n = D[r].transpose(0, 2, 1); lev = np.searchsorted(START, n, side="right"); who = (n - START[lev - 1]) // SIZE[lev - 1]
                key = rng.random((8, m, 16)) + bias(d, r, lev, who)
                pick = rng.permuted(np.argsort(key.reshape(8, -1), axis=1)[:, :m2], axis=1)
                p = pick >> 4; c = pick & 15
                par[r, :, o2 - LPR:o2 - LPR + m2] = p; let[r, :, o2 - LPR:o2 - LPR + m2] = c
                own[A8, c, p] = b2 + r * m2 + np.arange(m2)
                new.append(D[r][A8, c, p])
            G[:, :, b + r * m:b + (r + 1) * m] = np.where(own != 0, own, D[r])
        D = [np.take_along_axis(G, fl[:, None, :], 2) for fl in new]
    return tri, par, let, G
def walk(rng, G, go):
    txt = np.zeros((N, 8, ST, S), np.int64); s = np.zeros((N, 8, S), np.int64)
    for t in range(ST):
        col = G[np.arange(8)[None, :, None], :, s]
        c = np.argmax(rng.random(col.shape) + (col > s[..., None]) * (rng.random((N, 8, S, 1)) < go[..., None]), axis=-1)
        txt[:, :, t] = c; s = np.take_along_axis(col, c[..., None], 3)[..., 0]
    return txt
def pack(tri, par, let, txt):
    return {"tri": np.ascontiguousarray(tri.reshape(N, 128, C)).astype(np.int32), "par": np.stack([gtable(a) for a in par]),
            "let": let.astype(np.int32), "txt": np.ascontiguousarray(txt.reshape(N, 8, ST * S)).astype(np.int32)}
def setup_inputs(rng):
    pull = rng.choice(np.array([0.0, 0.2, 0.5, 2.0]), (N, 8, 1, 1))
    tri, par, let, G = grow(rng, lambda d, r, lev, who: -pull[r] * lev)
    return pack(tri, par, let, walk(rng, G, rng.choice(np.array([0.3, 0.7, 0.95]), (N, 8, S))))
def setup_inputs_depth(rng):
    pull = np.where(rng.permutation(8) < 4, 4.0, -4.0).reshape(8, 1, 1)
    tri, par, let, G = grow(rng, lambda d, r, lev, who: -pull * lev)
    return pack(tri, par, let, walk(rng, G, rng.choice(np.array([0.5, 1.0, 1.0]), (N, 8, S))))
def setup_inputs_bushy(rng):
    def bias(d, r, lev, who):
        v = np.zeros(lev.shape); m = lev.shape[1]
        v[0::2] = 10.0 * np.argsort(rng.random((4, m)), axis=1)[:, :, None]
        v[1::2] = 10.0 * np.argsort(rng.random((4, m, 16)), axis=2)
        return v
    tri, par, let, G = grow(rng, bias)
    txt = walk(rng, G, rng.choice(np.array([0.2, 0.8, 1.0]), (N, 8, S)))
    for r in range(N):
        g = 2 * rng.permutation(4) + 1
        txt[r, g[0]] = (np.add.accumulate(rng.integers(1, 16, ST)) & 15)[:, None]
        txt[r, g[1]] = LPR * ((r + 1 + int(rng.integers(0, N - 1))) % N) + rng.integers(0, LPR, (ST, S))
    return pack(tri, par, let, txt)
def setup_inputs_ends(rng):
    def bias(d, r, lev, who):
        v = np.zeros(lev.shape); m = lev.shape[1]; p = np.arange(m); c = np.arange(16)
        v[0::2] = 100.0 * np.minimum(p, m - 1 - p)[None, :, None]
        v[1::2] = 10.0 * ((c != 0) & (c != 15))[None, None, :] - 0.5 * lev[1::2]
        return v
    tri, par, let, G = grow(rng, bias)
    txt = walk(rng, G, rng.choice(np.array([0.3, 0.7, 1.0]), (N, 8, S))); q = S >> 3
    txt[..., :q] = 0; txt[..., q:2 * q] = 15
    txt[..., 2 * q:3 * q] = (15 * (np.arange(ST) & 1))[None, None, :, None]
    txt[..., 3 * q:4 * q] = rng.integers(0, 16, (N, 8, 1, q)); txt[..., 4 * q:5 * q] = txt[..., 7 * q:7 * q + 1]
    return pack(tri, par, let, txt)
def setup_inputs_spread(rng):
    wt = np.stack([0.15 * rng.permutation(16) ** np.exp2(rng.integers(-1, 2)) for g in range(8)])[:, None, :]
    pull = rng.choice(np.array([-0.5, 0.0, 0.5, 3.0]), (len(LEV), N, 8, 1, 1)); q = int(rng.integers(0, N))
    tri, par, let, G = grow(rng, lambda d, r, lev, who: wt - pull[d, r] * lev + (100.0 if d == 2 else 0.0) * (who != q))
    txt = walk(rng, G, rng.random((N, 8, S)))
    odd = np.minimum((16 * rng.random((N, 8, ST, S)) ** np.exp2(rng.integers(-3, 4, (N, 8, 1, S)))).astype(np.int64), 15)
    return pack(tri, par, let, np.where(rng.random((N, 8, 1, S)) < 0.4, odd, txt))
def check_inputs(d):
    bad = []
    for k in ("let", "txt"):
        if np.min(d[k]) < 0 or np.max(d[k]) > 15: bad.append("range of " + k)
    par = np.stack([gentries(a) for a in d["par"]]).astype(np.int64); let = d["let"].astype(np.int64)
    for i in range(1, len(LEV)):
        m, o = LEV[i][1:]; part = par[:, :, o - LPR:o - LPR + m]
        if np.min(part) < 0 or np.max(part) >= LEV[i - 1][1]: bad.append("range of par on level " + str(i + 1))
    if bad: return bad
    want = np.zeros((N, 8, 16, C), np.int64)
    for i in range(1, len(LEV)):
        b, m, o = LEV[i]
        for r in range(N):
            want[r][A8, let[r, :, o - LPR:o - LPR + m], LEV[i - 1][2] + par[r, :, o - LPR:o - LPR + m]] = b + r * m + np.arange(m)
    if np.count_nonzero(want) != N * 8 * (C - LPR): bad.append("two states with one parent and letter")
    if not np.array_equal(want.reshape(N, 128, C), d["tri"]): bad.append("tri against par and let")
    return bad
def reference(tri, par, let, txt):
    t4 = tri.astype(np.int64).reshape(N, 8, 16, C); pl = np.stack([gentries(a) for a in par]).astype(np.int64)
    ll = let.astype(np.int64); tx = txt.astype(np.int64).reshape(N, 8, ST, S)
    G = np.zeros((8, 16, W), np.int64); G[:, :, 0] = 16 + np.arange(16)
    fail = np.zeros((8, W), np.int64)
    yg = np.zeros((N, 8, 16, C), np.int64); yf = np.zeros((N, 8, C), np.int64)
    for i in range(len(LEV)):
        b, m, o = LEV[i]
        for r in range(N):
            fl = np.zeros((8, m), np.int64)
            if i > 0:
                pb, pm = LEV[i - 1][:2]
                fp = np.take_along_axis(fail, pb + r * pm + pl[r, :, o - LPR:o - LPR + m], 1)
                fl = G[A8, ll[r, :, o - LPR:o - LPR + m], fp]
            own = t4[r, :, :, o:o + m]
            full = np.where(own != 0, own, np.take_along_axis(G, fl[:, None, :], 2))
            fail[:, b + r * m:b + (r + 1) * m] = fl; G[:, :, b + r * m:b + (r + 1) * m] = full
            yf[r, :, o:o + m] = fl; yg[r, :, :, o:o + m] = full
    s = np.zeros((N, 8, S), np.int64); big = np.zeros((N, 8, S), np.int64)
    for t in range(ST):
        s = G[np.arange(8)[None, :, None], tx[:, :, t], s]
        big = np.maximum(big, s)
    return {"yg": yg.reshape(N, 128, C).astype(np.float32), "yf": yf.astype(np.float32), "yl": s.astype(np.float32), "ym": big.astype(np.float32)}

@@ -1,0 +1,483 @@
+from concourse.bass import DstId, RemoteDMATransfer
+from concourse.mybir import AluOpType as A, ActivationFunctionType as F
+
+K = 0.008435
+A0 = 5256
+MAGIC = 12582912
+SIZE = {1: 4, 2: 64, 3: 512, 4: 512, 5: 512, 6: 512, 7: 512}
+OWN = {1: 0, 2: 4, 3: 68, 4: 580, 5: 1092, 6: 1604, 7: 2116}
+BASE = {1: 0, 2: 16, 3: 272, 4: 2320, 5: 4368, 6: 6416, 7: 8464, 8: 10512}
+SLOT = 72
+
+SCRATCH = {
+    "tab": ("sbuf", [128, 10512], "bfloat16"),
+    "ti12": ("sbuf", [128, 68], "int32"), "c12": ("sbuf", [128, 68], "float32"), "la": ("sbuf", [128, 4 * SLOT], "bfloat16"),
+    "leti": ("sbuf", [128, 164], "int32"), "letb": ("sbuf", [128, 164], "bfloat16"), "maskl": ("sbuf", [128, 2624], "bfloat16"),
+    "pari": ("sbuf", [128, 164], "int32"), "pu": ("sbuf", [128, 164], "uint16"),
+    "vi": ("sbuf", [128, 320], "int32"), "vb": ("sbuf", [128, 320], "bfloat16"), "vn": ("sbuf", [128, 320], "bfloat16"),
+    "vq": ("sbuf", [128, 320], "bfloat16"), "maskt": ("sbuf", [128, 4608], "bfloat16"),
+    "l2i": ("sbuf", [128, 4], "int32"), "fl2": ("sbuf", [128, 32], "uint16"), "d2": ("sbuf", [128, 64], "bfloat16"),
+    "lt": ("sbuf", [128, 320], "uint16"), "lnf": ("sbuf", [128, 164], "float32"), "lnt": ("sbuf", [128, 320], "float32"),
+    "mf": ("sbuf", [128, 164], "float32"), "mt": ("sbuf", [128, 320], "float32"), "rm": ("sbuf", [128, 320], "float32"),
+    "nf": ("sbuf", [128, 164], "float32"), "tr1": ("sbuf", [128, 128], "float32"), "tr2": ("sbuf", [128, 128], "float32"),
+    "oyl": ("sbuf", [128, 32], "float32"), "oym": ("sbuf", [128, 32], "float32"), "zz": ("sbuf", [128, 4], "float32"),
+    "ya": ("sbuf", [128, 2628], "float32"), "yb": ("sbuf", [128, 2628], "float32"), "yo": ("sbuf", [128, 2628], "float32"),
+    "ones": ("sbuf", [128, 128], "bfloat16"), "blk0": ("sbuf", [128, 128], "bfloat16"), "blk": ("sbuf", [128, 128], "bfloat16"),
+    "blk2": ("sbuf", [128, 128], "bfloat16"), "row2": ("sbuf", [128, 128], "bfloat16"),
+    "onesf": ("sbuf", [128, 128], "float32"), "ident": ("sbuf", [128, 128], "float32"),
+    "pcol": ("sbuf", [128, 1], "int32"), "cci": ("sbuf", [128, 1], "int32"), "ccf": ("sbuf", [128, 1], "float32"),
+    "cc2": ("sbuf", [128, 1], "float32"), "bq": ("sbuf", [128, 1], "float32"),
+    "row16": ("sbuf", [128, 16], "float32"), "ee": ("sbuf", [128, 16], "float32"),
+    "brd": ("sbuf", [128, 2048], "bfloat16"), "br2": ("sbuf", [128, 2048], "bfloat16"), "sel": ("sbuf", [128, 2048], "bfloat16"),
+}
+for _d in range(3, 7):
+    SCRATCH["ti%d" % _d] = ("sbuf", [128, 512], "int32")
+    SCRATCH["cf%d" % _d] = ("sbuf", [128, 512], "float32")
+    SCRATCH["tc%d" % _d] = ("sbuf", [128, 2048], "bfloat16")
+    SCRATCH["d%d" % _d] = ("sbuf", [128, 512], "bfloat16")
+for _d in range(3, 8):
+    SCRATCH["fl%d" % _d] = ("sbuf", [128, 128], "uint16")
+    SCRATCH["xf%d" % _d] = ("sbuf", [128, 512], "bfloat16")
+for _t in range(1, 10):
+    SCRATCH["xt%d" % _t] = ("sbuf", [128, 512], "bfloat16")
+for _b in ("pm0", "pm1", "pt0", "pt1", "pf0", "pf1", "px0", "px1"):
+    SCRATCH[_b] = ("psum", [128, 512], "float32")
+
+LOADS = ["ti12", "l2", "let", "ti3", "par", "txt", "ti4", "ti5", "ti6"]
+SEMAPHORES = (["v", "s", "p", "gc", "out", "sent", "a_f2", "a_t12"] + ["ld_" + n for n in LOADS]
+              + ["a_t%d" % d for d in range(3, 7)] + ["a_f%d" % d for d in range(3, 8)] + ["h%d" % d for d in range(4, 7)])
+
+
+def helper_of(core, ranks, topo):
+    for h in topo.cores_of(core):
+        if h != core and topo.die(h) != topo.die(core) and all(topo.may_write(h, r) for r in ranks if r != core):
+            return h
+    return None
+
+
+def bits(engines):
+    m = 0
+    for e in engines:
+        m |= 1 << e
+    return m
+
+
+def dst_id(c, topo):
+    rid, pid, _ = topo.addr(c)
+    return DstId(rid=rid, pnc=pid)
+
+
+def send(g, T, topo, core, dsts, ap, sem):
+    g.remote_dma_fused([RemoteDMATransfer(dst_ids=[dst_id(c, topo) for c in dsts], dma_engine_mask=topo.mask(core, dsts[0]),
+                                          remote_sem=T.sem[sem], srcs=[ap], dsts=[ap for c in dsts], alu_op=0)],
+                       local_sem=T.sem["sent"])
+    return len(topo.engines(core, dsts[0]))
+
+
+def helper_program(g, core, T, topo, r):
+    own = T.cores[r]
+    others = [c for c in T.cores if c != own]
+    near = spare_engines(own, core, others[0], topo)
+    n = 0
+    for d in range(4, 7):
+        g.wait_ge(T.sem["h%d" % d], len(near))
+        n += send(g, T, topo, core, others, T["tc%d" % d][:, 512 * r:512 * r + 512], "a_t%d" % d)
+    g.wait_ge(T.sem["sent"], n)
+
+
+def spare_engines(core, helper, other, topo):
+    far = set(topo.engines(core, other))
+    return [e for e in topo.engines(core, helper) if e not in far]
+
+
+def rank_program(g, core, T, topo):
+    rank = T.rank_of(core)
+    if rank is None:
+        for i, c in enumerate(T.cores):
+            if helper_of(c, T.cores, topo) == core:
+                helper_program(g, core, T, topo, i)
+        return
+    R = rank
+    others = [c for c in T.cores if c != core]
+    helper = helper_of(core, T.cores, topo)
+    queue = {"v": g.vector, "s": g.scalar, "p": g.tensor, "gc": g, "y": g.sync}
+    cnt = {"v": 0, "s": 0, "p": 0, "gc": 0, "out": 0, "sent": 0}
+    seen = {}
+
+    def wait(q, *hs):
+        for h in hs:
+            if h is None:
+                continue
+            sem, val = h
+            if seen.get((q, sem), 0) < val:
+                queue[q].wait_ge(T.sem[sem], val)
+                seen[(q, sem)] = val
+
+    def fin(q, ins):
+        cnt[q] += 1
+        ins.then_inc(T.sem[q], 1)
+        return (q, cnt[q])
+
+    V, S, P = g.vector, g.scalar, g.tensor
+    H = {}
+
+    def load(name, pairs):
+        for out, in_ in pairs:
+            g.sync.dma_start(out, in_).then_inc(T.sem["ld_" + name], 16)
+        H["ld_" + name] = ("ld_" + name, 16 * len(pairs))
+
+    load("ti12", [(T.ti12[:, :], T.tri[:, 0:68])])
+    load("l2", [(T.l2i[:, j:j + 1], T.let[:, 16 * j:16 * j + 16]) for j in range(4)])
+    load("let", [(T.leti[:, :], T.let[:, :])])
+    load("ti3", [(T.ti3[:, :], T.tri[:, OWN[3]:OWN[4]])])
+    load("par", [(T.pari[:, :], T.par[:, :])])
+    load("txt", [(T.vi[:, 32 * t:32 * t + 32], T.txt[:, 512 * t:512 * t + 512]) for t in range(10)])
+    for d in range(4, 7):
+        load("ti%d" % d, [(T["ti%d" % d][:, :], T.tri[:, OWN[d]:OWN[d + 1]])])
+
+    def store(out, in_, *hs):
+        wait("y", *hs)
+        g.sync.dma_start(out, in_).then_inc(T.sem["out"], 16)
+        cnt["out"] += 16
+
+    H["ones"] = fin("v", V.memset(T.ones[:, :], 1.0))
+    H["pcol"] = fin("gc", g.iota(T.pcol[:, :], [[0, 1]], 0, 1))
+    H["row16"] = fin("gc", g.iota(T.row16[:, :], [[1, 16]], 0, 0, allow_small_or_imprecise_dtypes=True))
+    wait("gc", H["ones"])
+    H["blk0"] = fin("gc", g.affine_select(T.blk0[:, :], T.ones[:, :], [[-16, 8], [0, 16]], A.is_ge, 0.0, 0, 1))
+    wait("gc", H["blk0"])
+    H["blk"] = fin("gc", g.affine_select(T.blk[:, :], T.blk0[:, :], [[16, 8], [0, 16]], A.is_ge, 0.0, 15, -1))
+    H["row2"] = fin("gc", g.iota(T.row2[:, :], [[0, 8], [2, 16]], 0, 0, allow_small_or_imprecise_dtypes=True))
+    H["sel0"] = fin("v", V.memset(T.sel[:, :], 0.0))
+    wait("v", H["pcol"])
+    h = fin("v", V.tensor_scalar(T.cci[:, :], T.pcol[:, :], 15, None, A.bitwise_and))
+    wait("v", h)
+    H["ccf"] = fin("v", V.tensor_copy(T.ccf[:, :], T.cci[:, :]))
+    wait("v", H["ccf"], H["row16"])
+    H["ee"] = fin("v", V.tensor_scalar(T.ee[:, :], T.row16[:, :], T.ccf[:, 0:1], None, A.is_equal))
+    h = fin("v", V.tensor_tensor(T.cc2[:, :], T.ccf[:, :], T.ccf[:, :], A.mult))
+    wait("v", h, H["ee"], H["blk"])
+    H["bq"] = fin("v", V.tensor_scalar(T.bq[:, :], T.cc2[:, :], -1.0, 1.0, A.mult, A.add))
+    wait("s", H["sel0"], H["blk"])
+    for i in range(16):
+        H["sel"] = fin("s", S.activation(T.sel[:, 129 * i:128 * (i + 1):16], T.blk[:, i:128:16], F.Copy))
+
+    def code(out, in_, *hs):
+        wait("s", *hs)
+        return fin("s", S.activation(out, in_, F.Exp, bias=-K * (16 + A0), scale=K))
+
+    wait("v", H["ld_ti12"])
+    H["c12"] = fin("v", V.tensor_copy(T.c12[:, :], T.ti12[:, :]))
+    H["e12"] = code(T.la[:, SLOT * R:SLOT * R + 68], T.c12[:, :], H["c12"])
+    wait("v", H["ld_l2"])
+    H["fl2"] = fin("v", V.tensor_copy(T.fl2[:, 8 * R:8 * R + 4], T.l2i[:, :]))
+    for i in range(16):
+        H["brd"] = fin("v", V.tensor_scalar(T.brd[:, 128 * i:128 * i + 128], T.blk[:, :], T.ee[:, i:i + 1], None, A.mult))
+
+    def out_to_ranks(ap, sem, *hs):
+        wait("gc", *hs)
+        cnt["sent"] += send(g, T, topo, core, others, ap, sem)
+        H[sem] = (sem, len(others) * len(topo.engines(core, others[0])))
+
+    out_to_ranks(T.la[:, SLOT * R:SLOT * R + 68], "a_t12", H["e12"])
+    out_to_ranks(T.fl2[:, 8 * R:8 * R + 4], "a_f2", H["fl2"])
+
+    def pointers(d):
+        wait("v", H["ld_ti%d" % d])
+        h = fin("v", V.tensor_copy(T["cf%d" % d][:, :], T["ti%d" % d][:, :]))
+        H["e%d" % d] = code(T["tc%d" % d][:, 512 * R:512 * R + 512], T["cf%d" % d][:, :], h)
+
+    pointers(3)
+    out_to_ranks(T.tc3[:, 512 * R:512 * R + 512], "a_t3", H["e3"])
+
+    def to_helper(d):
+        eng = spare_engines(core, helper, others[0], topo)
+        wait("gc", H["e%d" % d])
+        ap = T["tc%d" % d][:, 512 * R:512 * R + 512]
+        rid, pid, _ = topo.addr(helper)
+        g.remote_dma(ap, ap, T.sem["h%d" % d], T.sem["sent"], pid, rid, bits(eng))
+        cnt["sent"] += len(eng)
+        H["a_t%d" % d] = ("a_t%d" % d, len(others) * len(topo.engines(helper, others[0])))
+
+    last = {}
+
+    wait("v", H["ld_let"])
+    H["letb"] = fin("v", V.tensor_copy(T.letb[:, :], T.leti[:, :]))
+    wait("v", H["ld_par"])
+    H["pu"] = fin("v", V.tensor_copy(T.pu[:, :], T.pari[:, :]))
+
+    def let_pe(k):
+        b = "pm%d" % (k % 2)
+        wait("p", H["brd"], H["letb"], last.get(b))
+        for n, i in enumerate(range(3 * k, min(3 * k + 3, 16))):
+            H["letp%d" % k] = fin("p", P.matmul(T[b][:, 164 * n:164 * n + 164], T.brd[:, 128 * i:128 * i + 128], T.letb[:, :], True, True))
+
+    def let_mask(k):
+        b = "pm%d" % (k % 2)
+        n = 164 * (min(3 * k + 3, 16) - 3 * k)
+        wait("v", H["letp%d" % k], H["ccf"])
+        last[b] = H["ml%d" % k] = fin("v", V.tensor_scalar(T.maskl[:, 492 * k:492 * k + n], T[b][:, 0:n], T.ccf[:, 0:1], None, A.is_equal))
+
+    def let_seg(d):
+        lo, hi = OWN[d] - 4, OWN[d] - 4 + 512
+        return [H["ml%d" % k] for k in range(6) if 492 * k < hi and 492 * (k + 1) > lo]
+
+    tn = [0]
+
+    def text_mask(i, t0, t1):
+        b = "pt%d" % (tn[0] % 2)
+        tn[0] += 1
+        n = 32 * (t1 - t0)
+        wait("p", H["br2"], H["brd"], H["vq"], last.get(b))
+        P.matmul(T[b][:, 0:n], T.br2[:, 128 * i:128 * i + 128], T.vb[:, 32 * t0:32 * t1], True, False).then_inc(T.sem["p"], 1)
+        cnt["p"] += 1
+        h = fin("p", P.matmul(T[b][:, 0:n], T.brd[:, 128 * i:128 * i + 128], T.vq[:, 32 * t0:32 * t1], False, True))
+        wait("s", h, H["bq"])
+        o = 512 * (t0 - 1)
+        last[b] = H["mt%d" % t0] = fin("s", S.activation(T.maskt[:, o + i:o + 16 * n:16], T[b][:, 0:n], F.Relu, bias=T.bq[:, 0:1]))
+
+    wait("v", H["ld_txt"])
+    H["vb"] = fin("v", V.tensor_copy(T.vb[:, :], T.vi[:, :]))
+    h = fin("v", V.tensor_scalar(T.vn[:, :], T.vi[:, :], -1.0, None, A.mult))
+    wait("v", H["row2"])
+    h2 = fin("v", V.tensor_tensor(T.blk2[:, :], T.blk[:, :], T.row2[:, :], A.mult))
+    wait("v", h, H["vb"])
+    H["vq"] = fin("v", V.tensor_tensor(T.vq[:, :], T.vn[:, :], T.vb[:, :], A.mult))
+    wait("v", h2)
+    for i in range(16):
+        H["br2"] = fin("v", V.tensor_scalar(T.br2[:, 128 * i:128 * i + 128], T.blk2[:, :], T.ee[:, i:i + 1], None, A.mult))
+    H["lt0"] = fin("v", V.tensor_copy(T.lt[:, 0:32], T.vi[:, 0:32]))
+    let_pe(0)
+    let_pe(1)
+    pointers(4)
+    to_helper(4)
+    for i in range(16):
+        text_mask(i, 1, 4)
+    let_mask(0)
+    let_mask(1)
+    let_pe(2)
+    let_pe(3)
+    pointers(5)
+    to_helper(5)
+    pointers(6)
+    to_helper(6)
+    H["rm0"] = fin("v", V.tensor_scalar(T.rm[:, 0:32], T.vi[:, 0:32], float(MAGIC), None, A.add))
+    H["nf2"] = fin("v", V.tensor_scalar(T.nf[:, 0:4], T.l2i[:, :], 16.0, None, A.add))
+    H["zz"] = fin("v", V.memset(T.zz[0:8, :], 0.0))
+    H["onesf"] = fin("v", V.memset(T.onesf[:, :], 1.0))
+
+    def sums(bank, x, hx):
+        wait("p", hx, H["sel"], last.get(bank))
+        for i in range(16):
+            h = fin("p", P.matmul(T[bank][:, 32 * i:32 * i + 32] if False else T[bank][:, 0:32], T.sel[:, 128 * i:128 * i + 128],
+                                  T[x][:, i:512:16], i == 0, i == 15))
+        return h
+
+    def fail_gather(d):
+        q = OWN[d] - 4
+        wait("v", H["d%d" % (d - 1)], H["pu"], *let_seg(d))
+        h = fin("v", V.tensor_tensor(T["xf%d" % d][:, :], T["d%d" % (d - 1)][:, :].indirect(T.pu[:, q // 16:q // 16 + 32]),
+                                     T.maskl[:, q:q + 512], A.mult))
+        H["xf%d" % d] = sums("pf%d" % (d % 2), "xf%d" % d, h)
+
+    def fail_ln(d):
+        j = (OWN[d] - 4) // 16
+        wait("s", H["xf%d" % d])
+        last["pf%d" % (d % 2)] = H["lnf%d" % d] = fin("s", S.activation(T.lnf[:, j:j + 32], T["pf%d" % (d % 2)][:, 0:32], F.Ln))
+
+    def fail_list(d):
+        j = (OWN[d] - 4) // 16
+        wait("v", H["lnf%d" % d])
+        H["mf%d" % d] = fin("v", V.tensor_scalar(T.mf[:, j:j + 32], T.lnf[:, j:j + 32], 1.0 / K, float(MAGIC + A0), A.mult, A.add))
+        wait("v", H["mf%d" % d])
+        ap = T["fl%d" % d][:, 32 * R:32 * R + 32]
+        H["fl%d" % d] = fin("v", V.tensor_scalar(ap, T.mf[:, j:j + 32], -float(MAGIC), None, A.add))
+        out_to_ranks(ap, "a_f%d" % d, H["fl%d" % d])
+
+    def text_gather(t):
+        wait("v", H["lt%d" % (t - 1)], H["tab%d" % min(t, 7)], H["mt1" if t < 4 else "mt4"])
+        if t >= 7:
+            wait("v", *H["tab7s"])
+        h = fin("v", V.tensor_tensor(T["xt%d" % t][:, :], T.tab[:, 0:BASE[min(t, 7) + 1]].indirect(T.lt[:, 32 * t - 32:32 * t]),
+                                     T.maskt[:, 512 * t - 512:512 * t], A.mult))
+        H["xt%d" % t] = sums("px%d" % (t % 2), "xt%d" % t, h)
+
+    def text_ln(t):
+        wait("s", H["xt%d" % t])
+        last["px%d" % (t % 2)] = H["lnt%d" % t] = fin("s", S.activation(T.lnt[:, 32 * t:32 * t + 32], T["px%d" % (t % 2)][:, 0:32], F.Ln))
+
+    def text_list(t):
+        c = slice(32 * t, 32 * t + 32)
+        wait("v", H["lnt%d" % t])
+        h = fin("v", V.tensor_scalar(T.mt[:, c], T.lnt[:, c], 1.0 / K, float(MAGIC + A0), A.mult, A.add))
+        wait("v", h)
+        if t < 9:
+            H["lt%d" % t] = fin("v", V.tensor_scalar(T.lt[:, c], T.mt[:, c], -float(MAGIC), None, A.add))
+        else:
+            H["oyl"] = fin("v", V.tensor_scalar(T.oyl[:, :], T.mt[:, c], 16.0 - MAGIC, None, A.add))
+        wait("v", H["rm%d" % (t - 1)])
+        H["rm%d" % t] = fin("v", V.tensor_tensor(T.rm[:, c], T.rm[:, 32 * t - 32:32 * t], T.mt[:, c], A.max))
+
+    def fail_columns(d):
+        m = SIZE[d]
+        wait("s", H["tab%d" % (d - 1)], H["fl%d" % d])
+        off = T.fl2[:, 8 * R:8 * R + 4] if d == 2 else T["fl%d" % d][:, 32 * R:32 * R + 32]
+        H["d%d" % d] = fin("s", S.activation(T["d%d" % d][:, 0:m], T.tab[:, 0:BASE[d]].indirect(off), F.Copy))
+
+    def complete(d, r0, r1):
+        if r0 < r1:
+            return fin("v", V.tensor_tensor(T.tab[:, BASE[d] + 512 * r0:BASE[d] + 512 * r1],
+                                            T.tab[:, 0:BASE[d]].indirect(T["fl%d" % d][:, 32 * r0:32 * r1]),
+                                            T["tc%d" % d][:, 512 * r0:512 * r1], A.max))
+        return None
+
+    def complete_own(d):
+        wait("v", H["tab%d" % (d - 1)], H["fl%d" % d], H["e%d" % d])
+        H["own%d" % d] = complete(d, R, R + 1)
+
+    def complete_others(d):
+        wait("v", H["a_f%d" % d], H["a_t%d" % d])
+        hs = [complete(d, 0, R), complete(d, R + 1, 4)]
+        H["tab%d" % d] = [h for h in hs if h is not None][-1]
+
+    def own_ap(d):
+        return T.tab[:, BASE[d] + SIZE[d] * R:BASE[d] + SIZE[d] * R + SIZE[d]]
+
+    def yg_ln(d):
+        c = slice(OWN[d], OWN[d] + SIZE[d])
+        wait("s", H["own%d" % d])
+        H["ya%d" % d] = fin("s", S.activation(T.ya[:, c], own_ap(d), F.Ln))
+
+    def yg_round(d):
+        c = slice(OWN[d], OWN[d] + SIZE[d])
+        wait("s", H["ya%d" % d])
+        H["yb%d" % d] = fin("s", S.activation(T.yb[:, c], T.ya[:, c], F.Identity, bias=float(MAGIC + A0), scale=1.0 / K))
+
+    def yg_out(d):
+        c = slice(OWN[d], OWN[d] + SIZE[d])
+        wait("s", H["yb%d" % d])
+        h = fin("s", S.activation(T.yo[:, c], T.yb[:, c], F.Identity, bias=16.0 - MAGIC))
+        store(T.yg[:, c], T.yo[:, c], h)
+
+    def yf_numbers(j0, j1, hs):
+        wait("v", *hs)
+        a = 4 if j0 == 0 else j0
+        return fin("v", V.tensor_scalar(T.nf[:, a:j1], T.mf[:, a:j1], 16.0 - MAGIC, None, A.add))
+
+    def yf_turn(bank, j0, j1, h):
+        wait("p", h, H["nf2"], H["ident"], last.get(bank))
+        return fin("p", P.transpose(T[bank][0:j1 - j0, 0:128], T.nf[:, j0:j1], T.ident[:, :]))
+
+    def yf_out(bank, buf, j0, j1, h):
+        n = j1 - j0
+        wait("s", h)
+        h = fin("s", S.activation(T[buf][0:n, :], T[bank][0:n, 0:128], F.Copy))
+        for k in range(8):
+            store(T.yf[k:k + 1, 4 + 16 * j0:4 + 16 * j1], T[buf][0:n, 16 * k:16 * k + 16], h)
+
+    wait("v", H["a_t12"], H["e12"])
+    for r in range(4):
+        H["tab1"] = fin("v", V.tensor_copy(T.tab[:, 4 * r:4 * r + 4], T.la[:, SLOT * r:SLOT * r + 4]))
+    fail_columns(2)
+    wait("v", H["tab1"], H["a_f2"], H["fl2"])
+    for r in [R] + [r for r in range(4) if r != R]:
+        h = fin("v", V.tensor_tensor(T.tab[:, 16 + 64 * r:80 + 64 * r], T.tab[:, 0:16].indirect(T.fl2[:, 8 * r:8 * r + 4]),
+                                     T.la[:, SLOT * r + 4:SLOT * r + 68], A.max))
+        if r == R:
+            H["own2"] = h
+    H["tab2"] = h
+    store(T.yg[:, 0:4], T.c12[:, 0:4], H["c12"])
+    store(T.yf[:, 0:4], T.zz[0:8, :], H["zz"])
+    fail_gather(3)
+    yg_ln(2)
+    let_mask(2)
+    let_mask(3)
+    fail_ln(3)
+    fail_list(3)
+    wait("gc", H["onesf"])
+    H["ident"] = fin("gc", g.affine_select(T.ident[:, :], T.onesf[:, :], [[-1, 128]], A.is_equal, 0.0, 0, 1))
+    fail_columns(3)
+    text_gather(1)
+    let_pe(4)
+    let_pe(5)
+    complete_own(3)
+    yg_round(2)
+    yg_out(2)
+    text_ln(1)
+    fail_gather(4)
+    for i in range(0, 4):
+        text_mask(i, 4, 10)
+    text_list(1)
+    text_gather(2)
+    let_mask(4)
+    let_mask(5)
+    fail_ln(4)
+    fail_list(4)
+    for i in range(4, 8):
+        text_mask(i, 4, 10)
+    text_ln(2)
+    complete_others(3)
+    text_list(2)
+    for d in range(4, 7):
+        fail_columns(d)
+        complete_own(d)
+        fail_gather(d + 1)
+        yg_ln(d - 1)
+        yg_round(d - 1)
+        text_gather(d - 1)
+        fail_ln(d + 1)
+        fail_list(d + 1)
+        if d == 4:
+            for i in range(8, 16):
+                text_mask(i, 4, 10)
+        text_ln(d - 1)
+        yg_out(d - 1)
+        if d == 6:
+            h = yf_numbers(0, 100, [H["mf5"]])
+            h = yf_turn("pm0", 0, 100, h)
+        complete_others(d)
+        if d == 6:
+            yf_out("pm0", "tr1", 0, 100, h)
+        text_list(d - 1)
+    wait("s", H["tab6"], H["fl7"])
+
+    def plain(q, r):
+        out = T.tab[:, BASE[7] + 512 * r:BASE[7] + 512 * r + 512]
+        src = T.tab[:, 0:BASE[7]].indirect(T.fl7[:, 32 * r:32 * r + 32])
+        if q == "s":
+            return fin("s", S.activation(out, src, F.Copy))
+        return fin("v", V.tensor_copy(out, src))
+
+    H["own7"] = plain("s", R)
+    text_gather(6)
+    yg_ln(6)
+    text_ln(6)
+    text_list(6)
+    rest = [r for r in range(4) if r != R]
+    wait("s", H["a_f7"])
+    wait("v", H["a_f7"])
+    H["tab7s"] = [H["own7"], plain("s", rest[0])]
+    plain("v", rest[1])
+    H["tab7"] = plain("v", rest[2])
+    text_gather(7)
+    yg_round(6)
+    yg_out(6)
+    h7 = yf_numbers(100, 164, [H["mf6"], H["mf7"]])
+    text_ln(7)
+    text_list(7)
+    text_gather(8)
+    h7 = yf_turn("pm1", 100, 164, h7)
+    yg_ln(7)
+    yf_out("pm1", "tr2", 100, 164, h7)
+    text_ln(8)
+    text_list(8)
+    text_gather(9)
+    yg_round(7)
+    yg_out(7)
+    text_ln(9)
+    text_list(9)
+    store(T.yl[:, :], T.oyl[:, :], H["oyl"])
+    wait("v", H["rm9"])
+    h = fin("v", V.tensor_scalar(T.oym[:, :], T.rm[:, 288:320], 16.0 - MAGIC, None, A.add))
+    store(T.ym[:, :], T.oym[:, :], h)
+    wait("gc", ("v", cnt["v"]), ("s", cnt["s"]), ("p", cnt["p"]), ("gc", cnt["gc"]), ("out", cnt["out"]), ("sent", cnt["sent"]))

@@ -3,24 +3,29 @@ from concourse.mybir import AluOpType as A, ActivationFunctionType as F
 
 K = 0.008435
 A0 = 5256
+NONE = 6e-20
 MAGIC = 12582912
 SIZE = {1: 4, 2: 64, 3: 512, 4: 512, 5: 512, 6: 512, 7: 512}
 OWN = {1: 0, 2: 4, 3: 68, 4: 580, 5: 1092, 6: 1604, 7: 2116}
-BASE = {1: 0, 2: 16, 3: 272, 4: 2320, 5: 4368, 6: 6416, 7: 8464, 8: 10512}
+BASE = {1: 0, 2: 16, 3: 272, 4: 2320, 5: 4368, 6: 6416, 7: 8464}
 SLOT = 72
+PAD = {3: 0, 4: 0, 5: 0, 6: 16}
 
 SCRATCH = {
-    "tab": ("sbuf", [128, 10512], "bfloat16"),
-    "ti12": ("sbuf", [128, 68], "int32"), "c12": ("sbuf", [128, 68], "float32"), "la": ("sbuf", [128, 4 * SLOT], "bfloat16"),
+    "tab": ("sbuf", [128, 8464], "bfloat16"), "raw": ("sbuf", [128, 4 * SLOT], "int32"),
+    "c1f": ("sbuf", [128, 16], "float32"), "c2f": ("sbuf", [128, 256], "float32"), "c2": ("sbuf", [128, 256], "bfloat16"),
     "leti": ("sbuf", [128, 164], "int32"), "letb": ("sbuf", [128, 164], "bfloat16"), "maskl": ("sbuf", [128, 2624], "bfloat16"),
     "pari": ("sbuf", [128, 164], "int32"), "pu": ("sbuf", [128, 164], "uint16"),
-    "vi": ("sbuf", [128, 320], "int32"), "vb": ("sbuf", [128, 320], "bfloat16"), "vn": ("sbuf", [128, 320], "bfloat16"),
+    "vi": ("sbuf", [128, 320], "int32"), "vb": ("sbuf", [128, 320], "bfloat16"),
     "vq": ("sbuf", [128, 320], "bfloat16"), "maskt": ("sbuf", [128, 4608], "bfloat16"),
-    "l2i": ("sbuf", [128, 4], "int32"), "fl2": ("sbuf", [128, 32], "uint16"), "d2": ("sbuf", [128, 64], "bfloat16"),
-    "lt": ("sbuf", [128, 320], "uint16"), "lnf": ("sbuf", [128, 164], "float32"), "lnt": ("sbuf", [128, 320], "float32"),
-    "mf": ("sbuf", [128, 164], "float32"), "mt": ("sbuf", [128, 320], "float32"), "rm": ("sbuf", [128, 320], "float32"),
+    "fl2": ("sbuf", [128, 16], "uint16"), "d2": ("sbuf", [128, 64], "bfloat16"),
+    "lt": ("sbuf", [128, 320], "uint16"), "ltp": ("sbuf", [128, 320], "uint16"), "flp": ("sbuf", [128, 32], "uint16"),
+    "lnf": ("sbuf", [128, 164], "float32"), "lnt": ("sbuf", [128, 320], "float32"), "lnp": ("sbuf", [128, 320], "float32"),
+    "rm": ("sbuf", [128, 32], "float32"), "last": ("sbuf", [128, 64], "float32"), "lastm": ("sbuf", [128, 64], "float32"),
+    "oy": ("sbuf", [128, 64], "float32"),
     "nf": ("sbuf", [128, 164], "float32"), "tr1": ("sbuf", [128, 128], "float32"), "tr2": ("sbuf", [128, 128], "float32"),
-    "oyl": ("sbuf", [128, 32], "float32"), "oym": ("sbuf", [128, 32], "float32"), "zz": ("sbuf", [128, 4], "float32"),
+    "zz": ("sbuf", [128, 4], "float32"), "g6": ("sbuf", [128, 512], "bfloat16"),
+    "h7": ("sbuf", [128, 512], "bfloat16"), "g7": ("sbuf", [128, 512], "bfloat16"),
     "ya": ("sbuf", [128, 2628], "float32"), "yb": ("sbuf", [128, 2628], "float32"), "yo": ("sbuf", [128, 2628], "float32"),
     "ones": ("sbuf", [128, 128], "bfloat16"), "blk0": ("sbuf", [128, 128], "bfloat16"), "blk": ("sbuf", [128, 128], "bfloat16"),
     "blk2": ("sbuf", [128, 128], "bfloat16"), "row2": ("sbuf", [128, 128], "bfloat16"),
@@ -33,19 +38,22 @@ SCRATCH = {
 for _d in range(3, 7):
     SCRATCH["ti%d" % _d] = ("sbuf", [128, 512], "int32")
     SCRATCH["cf%d" % _d] = ("sbuf", [128, 512], "float32")
-    SCRATCH["tc%d" % _d] = ("sbuf", [128, 2048], "bfloat16")
+    SCRATCH["tc%d" % _d] = ("sbuf", [128, PAD[_d] + 2048], "bfloat16")
+for _d in range(3, 6):
     SCRATCH["d%d" % _d] = ("sbuf", [128, 512], "bfloat16")
 for _d in range(3, 8):
     SCRATCH["fl%d" % _d] = ("sbuf", [128, 128], "uint16")
     SCRATCH["xf%d" % _d] = ("sbuf", [128, 512], "bfloat16")
 for _t in range(1, 10):
     SCRATCH["xt%d" % _t] = ("sbuf", [128, 512], "bfloat16")
+for _t in range(6, 10):
+    SCRATCH["xp%d" % _t] = ("sbuf", [128, 512], "bfloat16")
 for _b in ("pm0", "pm1", "pt0", "pt1", "pf0", "pf1", "px0", "px1"):
     SCRATCH[_b] = ("psum", [128, 512], "float32")
 
-LOADS = ["ti12", "l2", "let", "ti3", "par", "txt", "ti4", "ti5", "ti6"]
-SEMAPHORES = (["v", "s", "p", "gc", "out", "sent", "a_f2", "a_t12"] + ["ld_" + n for n in LOADS]
-              + ["a_t%d" % d for d in range(3, 7)] + ["a_f%d" % d for d in range(3, 8)] + ["h%d" % d for d in range(4, 7)])
+LOADS = ["ti12", "let", "ti3", "par", "txt", "ti4", "ti5", "ti6"]
+SEMAPHORES = (["v", "s", "p", "gc", "out", "sent", "a_raw"] + ["ld_" + n for n in LOADS]
+              + ["a_t%d" % d for d in range(3, 7)] + ["a_f%d" % d for d in range(3, 7)] + ["h%d" % d for d in range(4, 7)])
 
 
 def helper_of(core, ranks, topo):
@@ -81,7 +89,7 @@ def helper_program(g, core, T, topo, r):
     n = 0
     for d in range(4, 7):
         g.wait_ge(T.sem["h%d" % d], len(near))
-        n += send(g, T, topo, core, others, T["tc%d" % d][:, 512 * r:512 * r + 512], "a_t%d" % d)
+        n += send(g, T, topo, core, others, T["tc%d" % d][:, PAD[d] + 512 * r:PAD[d] + 512 * r + 512], "a_t%d" % d)
     g.wait_ge(T.sem["sent"], n)
 
 
@@ -126,14 +134,15 @@ def rank_program(g, core, T, topo):
             g.sync.dma_start(out, in_).then_inc(T.sem["ld_" + name], 16)
         H["ld_" + name] = ("ld_" + name, 16 * len(pairs))
 
-    load("ti12", [(T.ti12[:, :], T.tri[:, 0:68])])
-    load("l2", [(T.l2i[:, j:j + 1], T.let[:, 16 * j:16 * j + 16]) for j in range(4)])
-    load("let", [(T.leti[:, :], T.let[:, :])])
+    slot = SLOT * R
+    load("ti12", [(T.raw[:, slot:slot + 68], T.tri[:, 0:68])]
+         + [(T.raw[:, slot + 68 + j:slot + 69 + j], T.let[:, 16 * j:16 * j + 16]) for j in range(4)])
     load("ti3", [(T.ti3[:, :], T.tri[:, OWN[3]:OWN[4]])])
+    load("let", [(T.leti[:, :], T.let[:, :])])
     load("par", [(T.pari[:, :], T.par[:, :])])
-    load("txt", [(T.vi[:, 32 * t:32 * t + 32], T.txt[:, 512 * t:512 * t + 512]) for t in range(10)])
     for d in range(4, 7):
         load("ti%d" % d, [(T["ti%d" % d][:, :], T.tri[:, OWN[d]:OWN[d + 1]])])
+    load("txt", [(T.vi[:, 32 * t:32 * t + 32], T.txt[:, 512 * t:512 * t + 512]) for t in range(10)])
 
     def store(out, in_, *hs):
         wait("y", *hs)
@@ -147,7 +156,7 @@ def rank_program(g, core, T, topo):
     H["blk0"] = fin("gc", g.affine_select(T.blk0[:, :], T.ones[:, :], [[-16, 8], [0, 16]], A.is_ge, 0.0, 0, 1))
     wait("gc", H["blk0"])
     H["blk"] = fin("gc", g.affine_select(T.blk[:, :], T.blk0[:, :], [[16, 8], [0, 16]], A.is_ge, 0.0, 15, -1))
-    H["row2"] = fin("gc", g.iota(T.row2[:, :], [[0, 8], [2, 16]], 0, 0, allow_small_or_imprecise_dtypes=True))
+    H["row2"] = fin("gc", g.iota(T.row2[:, :], [[0, 8], [-2, 16]], 0, 0, allow_small_or_imprecise_dtypes=True))
     H["sel0"] = fin("v", V.memset(T.sel[:, :], 0.0))
     wait("v", H["pcol"])
     h = fin("v", V.tensor_scalar(T.cci[:, :], T.pcol[:, :], 15, None, A.bitwise_and))
@@ -161,43 +170,43 @@ def rank_program(g, core, T, topo):
     wait("s", H["sel0"], H["blk"])
     for i in range(16):
         H["sel"] = fin("s", S.activation(T.sel[:, 129 * i:128 * (i + 1):16], T.blk[:, i:128:16], F.Copy))
+    for i in range(16):
+        H["brd"] = fin("v", V.tensor_scalar(T.brd[:, 128 * i:128 * i + 128], T.blk[:, :], T.ee[:, i:i + 1], None, A.mult))
+    wait("v", H["row2"])
+    h2 = fin("v", V.tensor_tensor(T.blk2[:, :], T.blk[:, :], T.row2[:, :], A.mult))
+    H["fill"] = fin("v", V.memset(T.tc6[:, 0:PAD[6]], NONE))
+    wait("v", h2)
+    for i in range(16):
+        H["br2"] = fin("v", V.tensor_scalar(T.br2[:, 128 * i:128 * i + 128], T.blk2[:, :], T.ee[:, i:i + 1], None, A.mult))
 
     def code(out, in_, *hs):
         wait("s", *hs)
         return fin("s", S.activation(out, in_, F.Exp, bias=-K * (16 + A0), scale=K))
-
-    wait("v", H["ld_ti12"])
-    H["c12"] = fin("v", V.tensor_copy(T.c12[:, :], T.ti12[:, :]))
-    H["e12"] = code(T.la[:, SLOT * R:SLOT * R + 68], T.c12[:, :], H["c12"])
-    wait("v", H["ld_l2"])
-    H["fl2"] = fin("v", V.tensor_copy(T.fl2[:, 8 * R:8 * R + 4], T.l2i[:, :]))
-    for i in range(16):
-        H["brd"] = fin("v", V.tensor_scalar(T.brd[:, 128 * i:128 * i + 128], T.blk[:, :], T.ee[:, i:i + 1], None, A.mult))
 
     def out_to_ranks(ap, sem, *hs):
         wait("gc", *hs)
         cnt["sent"] += send(g, T, topo, core, others, ap, sem)
         H[sem] = (sem, len(others) * len(topo.engines(core, others[0])))
 
-    out_to_ranks(T.la[:, SLOT * R:SLOT * R + 68], "a_t12", H["e12"])
-    out_to_ranks(T.fl2[:, 8 * R:8 * R + 4], "a_f2", H["fl2"])
+    def own_tc(d):
+        return T["tc%d" % d][:, PAD[d] + 512 * R:PAD[d] + 512 * R + 512]
 
     def pointers(d):
         wait("v", H["ld_ti%d" % d])
         h = fin("v", V.tensor_copy(T["cf%d" % d][:, :], T["ti%d" % d][:, :]))
-        H["e%d" % d] = code(T["tc%d" % d][:, 512 * R:512 * R + 512], T["cf%d" % d][:, :], h)
-
-    pointers(3)
-    out_to_ranks(T.tc3[:, 512 * R:512 * R + 512], "a_t3", H["e3"])
+        H["e%d" % d] = code(own_tc(d), T["cf%d" % d][:, :], h)
 
     def to_helper(d):
         eng = spare_engines(core, helper, others[0], topo)
         wait("gc", H["e%d" % d])
-        ap = T["tc%d" % d][:, 512 * R:512 * R + 512]
         rid, pid, _ = topo.addr(helper)
-        g.remote_dma(ap, ap, T.sem["h%d" % d], T.sem["sent"], pid, rid, bits(eng))
+        g.remote_dma(own_tc(d), own_tc(d), T.sem["h%d" % d], T.sem["sent"], pid, rid, bits(eng))
         cnt["sent"] += len(eng)
         H["a_t%d" % d] = ("a_t%d" % d, len(others) * len(topo.engines(helper, others[0])))
+
+    out_to_ranks(T.raw[:, slot:slot + SLOT], "a_raw", H["ld_ti12"])
+    pointers(3)
+    out_to_ranks(own_tc(3), "a_t3", H["e3"])
 
     last = {}
 
@@ -205,15 +214,16 @@ def rank_program(g, core, T, topo):
     H["letb"] = fin("v", V.tensor_copy(T.letb[:, :], T.leti[:, :]))
     wait("v", H["ld_par"])
     H["pu"] = fin("v", V.tensor_copy(T.pu[:, :], T.pari[:, :]))
+    LB = ["pm0", "pm1", "px0", "px1", "pm0", "pm1"]
 
     def let_pe(k):
-        b = "pm%d" % (k % 2)
+        b = LB[k]
         wait("p", H["brd"], H["letb"], last.get(b))
         for n, i in enumerate(range(3 * k, min(3 * k + 3, 16))):
             H["letp%d" % k] = fin("p", P.matmul(T[b][:, 164 * n:164 * n + 164], T.brd[:, 128 * i:128 * i + 128], T.letb[:, :], True, True))
 
     def let_mask(k):
-        b = "pm%d" % (k % 2)
+        b = LB[k]
         n = 164 * (min(3 * k + 3, 16) - 3 * k)
         wait("v", H["letp%d" % k], H["ccf"])
         last[b] = H["ml%d" % k] = fin("v", V.tensor_scalar(T.maskl[:, 492 * k:492 * k + n], T[b][:, 0:n], T.ccf[:, 0:1], None, A.is_equal))
@@ -224,59 +234,57 @@ def rank_program(g, core, T, topo):
 
     tn = [0]
 
-    def text_mask(i, t0, t1):
+    def masks_pe(lo, hi, t0, t1):
         b = "pt%d" % (tn[0] % 2)
         tn[0] += 1
         n = 32 * (t1 - t0)
-        wait("p", H["br2"], H["brd"], H["vq"], last.get(b))
-        P.matmul(T[b][:, 0:n], T.br2[:, 128 * i:128 * i + 128], T.vb[:, 32 * t0:32 * t1], True, False).then_inc(T.sem["p"], 1)
-        cnt["p"] += 1
-        h = fin("p", P.matmul(T[b][:, 0:n], T.brd[:, 128 * i:128 * i + 128], T.vq[:, 32 * t0:32 * t1], False, True))
+        wait("p", H["br2"], H["brd"], H["vb"], H["vq"], last.get(b))
+        for m, i in enumerate(range(lo, hi)):
+            ap = T[b][:, m * n:m * n + n]
+            P.matmul(ap, T.br2[:, 128 * i:128 * i + 128], T.vb[:, 32 * t0:32 * t1], True, False).then_inc(T.sem["p"], 1)
+            cnt["p"] += 1
+            h = fin("p", P.matmul(ap, T.brd[:, 128 * i:128 * i + 128], T.vq[:, 32 * t0:32 * t1], False, True))
+        return (b, h, lo, hi, t0, n)
+
+    def masks_out(made):
+        b, h, lo, hi, t0, n = made
         wait("s", h, H["bq"])
         o = 512 * (t0 - 1)
-        last[b] = H["mt%d" % t0] = fin("s", S.activation(T.maskt[:, o + i:o + 16 * n:16], T[b][:, 0:n], F.Relu, bias=T.bq[:, 0:1]))
+        for m, i in enumerate(range(lo, hi)):
+            last[b] = H["mt%d" % t0] = fin("s", S.activation(T.maskt[:, o + i:o + 16 * n:16], T[b][:, m * n:m * n + n], F.Relu,
+                                                             bias=T.bq[:, 0:1], scale=-1.0))
 
-    wait("v", H["ld_txt"])
-    H["vb"] = fin("v", V.tensor_copy(T.vb[:, :], T.vi[:, :]))
-    h = fin("v", V.tensor_scalar(T.vn[:, :], T.vi[:, :], -1.0, None, A.mult))
-    wait("v", H["row2"])
-    h2 = fin("v", V.tensor_tensor(T.blk2[:, :], T.blk[:, :], T.row2[:, :], A.mult))
-    wait("v", h, H["vb"])
-    H["vq"] = fin("v", V.tensor_tensor(T.vq[:, :], T.vn[:, :], T.vb[:, :], A.mult))
-    wait("v", h2)
-    for i in range(16):
-        H["br2"] = fin("v", V.tensor_scalar(T.br2[:, 128 * i:128 * i + 128], T.blk2[:, :], T.ee[:, i:i + 1], None, A.mult))
-    H["lt0"] = fin("v", V.tensor_copy(T.lt[:, 0:32], T.vi[:, 0:32]))
+    def text_masks(*which):
+        masks_out(masks_pe(*which))
+
     let_pe(0)
     let_pe(1)
-    pointers(4)
-    to_helper(4)
-    for i in range(16):
-        text_mask(i, 1, 4)
-    let_mask(0)
-    let_mask(1)
     let_pe(2)
     let_pe(3)
+    pointers(4)
+    to_helper(4)
+    let_mask(0)
+    let_mask(1)
     pointers(5)
     to_helper(5)
     pointers(6)
     to_helper(6)
-    H["rm0"] = fin("v", V.tensor_scalar(T.rm[:, 0:32], T.vi[:, 0:32], float(MAGIC), None, A.add))
-    H["nf2"] = fin("v", V.tensor_scalar(T.nf[:, 0:4], T.l2i[:, :], 16.0, None, A.add))
-    H["zz"] = fin("v", V.memset(T.zz[0:8, :], 0.0))
-    H["onesf"] = fin("v", V.memset(T.onesf[:, :], 1.0))
 
     def sums(bank, x, hx):
         wait("p", hx, H["sel"], last.get(bank))
         for i in range(16):
-            h = fin("p", P.matmul(T[bank][:, 32 * i:32 * i + 32] if False else T[bank][:, 0:32], T.sel[:, 128 * i:128 * i + 128],
-                                  T[x][:, i:512:16], i == 0, i == 15))
+            h = fin("p", P.matmul(T[bank][:, 0:32], T.sel[:, 128 * i:128 * i + 128], T[x][:, i:512:16], i == 0, i == 15))
         return h
+
+    def fail_cols(d):
+        if d == 6:
+            return T.tab[:, BASE[6] + 512 * R:BASE[6] + 512 * R + 512]
+        return T["d%d" % d][:, :]
 
     def fail_gather(d):
         q = OWN[d] - 4
         wait("v", H["d%d" % (d - 1)], H["pu"], *let_seg(d))
-        h = fin("v", V.tensor_tensor(T["xf%d" % d][:, :], T["d%d" % (d - 1)][:, :].indirect(T.pu[:, q // 16:q // 16 + 32]),
+        h = fin("v", V.tensor_tensor(T["xf%d" % d][:, :], fail_cols(d - 1).indirect(T.pu[:, q // 16:q // 16 + 32]),
                                      T.maskl[:, q:q + 512], A.mult))
         H["xf%d" % d] = sums("pf%d" % (d % 2), "xf%d" % d, h)
 
@@ -285,20 +293,22 @@ def rank_program(g, core, T, topo):
         wait("s", H["xf%d" % d])
         last["pf%d" % (d % 2)] = H["lnf%d" % d] = fin("s", S.activation(T.lnf[:, j:j + 32], T["pf%d" % (d % 2)][:, 0:32], F.Ln))
 
+    def own_list(d):
+        return T["fl%d" % d][:, 32 * R:32 * R + 32]
+
     def fail_list(d):
         j = (OWN[d] - 4) // 16
         wait("v", H["lnf%d" % d])
-        H["mf%d" % d] = fin("v", V.tensor_scalar(T.mf[:, j:j + 32], T.lnf[:, j:j + 32], 1.0 / K, float(MAGIC + A0), A.mult, A.add))
-        wait("v", H["mf%d" % d])
-        ap = T["fl%d" % d][:, 32 * R:32 * R + 32]
-        H["fl%d" % d] = fin("v", V.tensor_scalar(ap, T.mf[:, j:j + 32], -float(MAGIC), None, A.add))
-        out_to_ranks(ap, "a_f%d" % d, H["fl%d" % d])
+        H["fl%d" % d] = fin("v", V.tensor_scalar(own_list(d), T.lnf[:, j:j + 32], 1.0 / K, float(A0), A.mult, A.add))
+        if d < 7:
+            out_to_ranks(own_list(d), "a_f%d" % d, H["fl%d" % d])
+        else:
+            H["flp"] = fin("v", V.tensor_scalar(T.flp[:, :], T.lnf[:, j:j + 32], 1.0 / K, float(A0 - BASE[6] + PAD[6]), A.mult, A.add))
 
     def text_gather(t):
-        wait("v", H["lt%d" % (t - 1)], H["tab%d" % min(t, 7)], H["mt1" if t < 4 else "mt4"])
-        if t >= 7:
-            wait("v", *H["tab7s"])
-        h = fin("v", V.tensor_tensor(T["xt%d" % t][:, :], T.tab[:, 0:BASE[min(t, 7) + 1]].indirect(T.lt[:, 32 * t - 32:32 * t]),
+        d = min(t, 6)
+        wait("v", H["lt%d" % (t - 1)], H["mt1" if t < 4 else "mt4"], *H["tab%d" % d])
+        h = fin("v", V.tensor_tensor(T["xt%d" % t][:, :], T.tab[:, 0:BASE[d + 1]].indirect(T.lt[:, 32 * t - 32:32 * t]),
                                      T.maskt[:, 512 * t - 512:512 * t], A.mult))
         H["xt%d" % t] = sums("px%d" % (t % 2), "xt%d" % t, h)
 
@@ -309,38 +319,75 @@ def rank_program(g, core, T, topo):
     def text_list(t):
         c = slice(32 * t, 32 * t + 32)
         wait("v", H["lnt%d" % t])
-        h = fin("v", V.tensor_scalar(T.mt[:, c], T.lnt[:, c], 1.0 / K, float(MAGIC + A0), A.mult, A.add))
-        wait("v", h)
-        if t < 9:
-            H["lt%d" % t] = fin("v", V.tensor_scalar(T.lt[:, c], T.mt[:, c], -float(MAGIC), None, A.add))
-        else:
-            H["oyl"] = fin("v", V.tensor_scalar(T.oyl[:, :], T.mt[:, c], 16.0 - MAGIC, None, A.add))
-        wait("v", H["rm%d" % (t - 1)])
-        H["rm%d" % t] = fin("v", V.tensor_tensor(T.rm[:, c], T.rm[:, 32 * t - 32:32 * t], T.mt[:, c], A.max))
+        H["lt%d" % t] = fin("v", V.tensor_scalar(T.lt[:, c], T.lnt[:, c], 1.0 / K, float(A0), A.mult, A.add))
+
+    def deep_list(t):
+        c = slice(32 * t, 32 * t + 32)
+        wait("v", H["lnt%d" % t])
+        H["ltp%d" % t] = fin("v", V.tensor_scalar(T.ltp[:, c], T.lnt[:, c], 1.0 / K, float(A0 - BASE[6] + PAD[6]), A.mult, A.add))
+
+    DB = {6: "pt0", 7: "pt1", 8: "pf0", 9: "pf1"}
+
+    def deep_gather(t):
+        wait("v", H["ltp%d" % (t - 1)], H["a_t6"], H["e6"], H["fill"])
+        h = fin("v", V.tensor_tensor(T["xp%d" % t][:, :], T.tc6[:, :].indirect(T.ltp[:, 32 * t - 32:32 * t]),
+                                     T.maskt[:, 512 * t - 512:512 * t], A.mult))
+        H["xp%d" % t] = sums(DB[t], "xp%d" % t, h)
+
+    def deep_ln(t):
+        wait("s", H["xp%d" % t])
+        last[DB[t]] = H["lnp%d" % t] = fin("s", S.activation(T.lnp[:, 32 * t:32 * t + 32], T[DB[t]][:, 0:32], F.Ln))
+
+    def running(*names):
+        for buf, t in names:
+            ap = T[buf][:, 32 * t:32 * t + 32]
+            wait("v", H["%s%d" % (buf, t)], H.get("rm"))
+            if "rm" in H:
+                H["rm"] = fin("v", V.tensor_tensor(T.rm[:, :], T.rm[:, :], ap, A.max))
+            else:
+                H["rm"] = fin("v", V.tensor_copy(T.rm[:, :], ap))
 
     def fail_columns(d):
-        m = SIZE[d]
-        wait("s", H["tab%d" % (d - 1)], H["fl%d" % d])
-        off = T.fl2[:, 8 * R:8 * R + 4] if d == 2 else T["fl%d" % d][:, 32 * R:32 * R + 32]
-        H["d%d" % d] = fin("s", S.activation(T["d%d" % d][:, 0:m], T.tab[:, 0:BASE[d]].indirect(off), F.Copy))
+        wait("s", *H["tab%d" % (d - 1)])
+        wait("s", H["fl%d" % d])
+        off = T.fl2[:, 4 * R:4 * R + 4] if d == 2 else own_list(d)
+        out = T.d2[:, :] if d == 2 else fail_cols(d)
+        H["d%d" % d] = fin("s", S.activation(out, T.tab[:, 0:BASE[d]].indirect(off), F.Copy))
 
-    def complete(d, r0, r1):
-        if r0 < r1:
-            return fin("v", V.tensor_tensor(T.tab[:, BASE[d] + 512 * r0:BASE[d] + 512 * r1],
-                                            T.tab[:, 0:BASE[d]].indirect(T["fl%d" % d][:, 32 * r0:32 * r1]),
-                                            T["tc%d" % d][:, 512 * r0:512 * r1], A.max))
-        return None
+    def complete(d, c0, c1):
+        if c0 < c1:
+            wait("v", *H["tab%d" % (d - 1)])
+            return [fin("v", V.tensor_tensor(T.tab[:, BASE[d] + 16 * c0:BASE[d] + 16 * c1],
+                                             T.tab[:, 0:BASE[d]].indirect(T["fl%d" % d][:, c0:c1]),
+                                             T["tc%d" % d][:, 16 * c0:16 * c1], A.max))]
+        return []
 
     def complete_own(d):
-        wait("v", H["tab%d" % (d - 1)], H["fl%d" % d], H["e%d" % d])
-        H["own%d" % d] = complete(d, R, R + 1)
+        wait("v", H["fl%d" % d], H["e%d" % d])
+        H["tab%d" % d] = complete(d, 32 * R, 32 * R + 32)
+        H["own%d" % d] = H["tab%d" % d][0]
 
-    def complete_others(d):
+    def complete_others(d, part):
         wait("v", H["a_f%d" % d], H["a_t%d" % d])
-        hs = [complete(d, 0, R), complete(d, R + 1, 4)]
-        H["tab%d" % d] = [h for h in hs if h is not None][-1]
+        cuts = [(0, 16), (16, 32 * R), (32 * R + 32, 128)] if R else [(32, 48), (48, 128)]
+        for c in (cuts[:1] if part == 0 else cuts[1:]):
+            H["tab%d" % d] += complete(d, *c)
+
+    def plain(q, r):
+        off = T.fl6[:, 32 * r:32 * r + 32]
+        out = T.tab[:, BASE[6] + 512 * r:BASE[6] + 512 * r + 512]
+        src = T.tab[:, 0:BASE[6]].indirect(off)
+        wait(q, *H["tab5"])
+        wait(q, H["a_f6"])
+        if q == "s":
+            h = fin("s", S.activation(out, src, F.Copy))
+        else:
+            h = fin("v", V.tensor_copy(out, src))
+        H["tab6"].append(h)
 
     def own_ap(d):
+        if d >= 6:
+            return T["g%d" % d][:, :]
         return T.tab[:, BASE[d] + SIZE[d] * R:BASE[d] + SIZE[d] * R + SIZE[d]]
 
     def yg_ln(d):
@@ -348,24 +395,26 @@ def rank_program(g, core, T, topo):
         wait("s", H["own%d" % d])
         H["ya%d" % d] = fin("s", S.activation(T.ya[:, c], own_ap(d), F.Ln))
 
+    def yg_cols(d):
+        return slice(0 if d == 2 else OWN[d], OWN[d] + SIZE[d])
+
     def yg_round(d):
-        c = slice(OWN[d], OWN[d] + SIZE[d])
         wait("s", H["ya%d" % d])
-        H["yb%d" % d] = fin("s", S.activation(T.yb[:, c], T.ya[:, c], F.Identity, bias=float(MAGIC + A0), scale=1.0 / K))
+        H["yb%d" % d] = fin("s", S.activation(T.yb[:, yg_cols(d)], T.ya[:, yg_cols(d)], F.Identity, bias=float(MAGIC + A0), scale=1.0 / K))
 
     def yg_out(d):
-        c = slice(OWN[d], OWN[d] + SIZE[d])
         wait("s", H["yb%d" % d])
-        h = fin("s", S.activation(T.yo[:, c], T.yb[:, c], F.Identity, bias=16.0 - MAGIC))
-        store(T.yg[:, c], T.yo[:, c], h)
+        h = fin("s", S.activation(T.yo[:, yg_cols(d)], T.yb[:, yg_cols(d)], F.Identity, bias=16.0 - MAGIC))
+        store(T.yg[:, yg_cols(d)], T.yo[:, yg_cols(d)], h)
 
-    def yf_numbers(j0, j1, hs):
-        wait("v", *hs)
-        a = 4 if j0 == 0 else j0
-        return fin("v", V.tensor_scalar(T.nf[:, a:j1], T.mf[:, a:j1], 16.0 - MAGIC, None, A.add))
+    def yf_numbers(d):
+        j = (OWN[d] - 4) // 16
+        wait("v", H["fl%d" % d])
+        H["nf%d" % d] = fin("v", V.tensor_scalar(T.nf[:, j:j + 32], own_list(d), 16.0, None, A.add))
 
-    def yf_turn(bank, j0, j1, h):
-        wait("p", h, H["nf2"], H["ident"], last.get(bank))
+    def yf_turn(bank, j0, j1, hs):
+        wait("p", *hs)
+        wait("p", H["ident"], last.get(bank))
         return fin("p", P.transpose(T[bank][0:j1 - j0, 0:128], T.nf[:, j0:j1], T.ident[:, :]))
 
     def yf_out(bank, buf, j0, j1, h):
@@ -375,109 +424,178 @@ def rank_program(g, core, T, topo):
         for k in range(8):
             store(T.yf[k:k + 1, 4 + 16 * j0:4 + 16 * j1], T[buf][0:n, 16 * k:16 * k + 16], h)
 
-    wait("v", H["a_t12"], H["e12"])
+    wait("v", H["a_raw"], H["ld_ti12"])
     for r in range(4):
-        H["tab1"] = fin("v", V.tensor_copy(T.tab[:, 4 * r:4 * r + 4], T.la[:, SLOT * r:SLOT * r + 4]))
+        h = fin("v", V.tensor_copy(T.c1f[:, 4 * r:4 * r + 4], T.raw[:, SLOT * r:SLOT * r + 4]))
+    H["tab1"] = [code(T.tab[:, 0:16], T.c1f[:, :], h)]
+    for r in range(4):
+        H["fl2"] = fin("v", V.tensor_copy(T.fl2[:, 4 * r:4 * r + 4], T.raw[:, SLOT * r + 68:SLOT * r + 72]))
     fail_columns(2)
-    wait("v", H["tab1"], H["a_f2"], H["fl2"])
-    for r in [R] + [r for r in range(4) if r != R]:
-        h = fin("v", V.tensor_tensor(T.tab[:, 16 + 64 * r:80 + 64 * r], T.tab[:, 0:16].indirect(T.fl2[:, 8 * r:8 * r + 4]),
-                                     T.la[:, SLOT * r + 4:SLOT * r + 68], A.max))
-        if r == R:
-            H["own2"] = h
-    H["tab2"] = h
-    store(T.yg[:, 0:4], T.c12[:, 0:4], H["c12"])
-    store(T.yf[:, 0:4], T.zz[0:8, :], H["zz"])
+    for r in range(4):
+        h = fin("v", V.tensor_copy(T.c2f[:, 64 * r:64 * r + 64], T.raw[:, SLOT * r + 4:SLOT * r + 68]))
+    H["c2"] = code(T.c2[:, :], T.c2f[:, :], h)
+    H["own1"] = H["tab1"][0]
+    yg_ln(1)
     fail_gather(3)
-    yg_ln(2)
-    let_mask(2)
-    let_mask(3)
+    wait("v", H["ld_txt"])
+    H["vb"] = fin("v", V.tensor_copy(T.vb[:, :], T.vi[:, :]))
+    wait("s", H["vb"])
+    H["vq"] = fin("s", S.activation(T.vq[:, :], T.vb[:, :], F.Square))
+    wait("v", H["c2"], *H["tab1"])
+    H["own2"] = fin("v", V.tensor_tensor(T.tab[:, 16:272], T.tab[:, 0:16].indirect(T.fl2[:, :]), T.c2[:, :], A.max))
+    H["tab2"] = [H["own2"]]
+    H["lt0"] = fin("v", V.tensor_copy(T.lt[:, 0:32], T.vi[:, 0:32]))
     fail_ln(3)
     fail_list(3)
-    wait("gc", H["onesf"])
-    H["ident"] = fin("gc", g.affine_select(T.ident[:, :], T.onesf[:, :], [[-1, 128]], A.is_equal, 0.0, 0, 1))
     fail_columns(3)
-    text_gather(1)
+    text_masks(0, 5, 1, 4)
+    text_masks(5, 10, 1, 4)
+    text_masks(10, 15, 1, 4)
+    text_masks(15, 16, 1, 4)
+    complete_own(3)
+    let_mask(2)
+    fail_gather(4)
+    let_mask(3)
     let_pe(4)
     let_pe(5)
-    complete_own(3)
-    yg_round(2)
-    yg_out(2)
-    text_ln(1)
-    fail_gather(4)
-    for i in range(0, 4):
-        text_mask(i, 4, 10)
-    text_list(1)
-    text_gather(2)
-    let_mask(4)
-    let_mask(5)
+    m0 = masks_pe(0, 2, 4, 10)
+    m1 = masks_pe(2, 4, 4, 10)
+    complete_others(3, 0)
+    text_gather(1)
     fail_ln(4)
     fail_list(4)
-    for i in range(4, 8):
-        text_mask(i, 4, 10)
+    masks_out(m0)
+    masks_out(m1)
+    text_ln(1)
+    complete_others(3, 1)
+    text_list(1)
+    fail_columns(4)
+    text_masks(4, 6, 4, 10)
+    text_masks(6, 8, 4, 10)
+    text_gather(2)
+    let_mask(4)
+    fail_gather(5)
     text_ln(2)
-    complete_others(3)
+    text_masks(8, 10, 4, 10)
+    m0 = masks_pe(10, 12, 4, 10)
+    m1 = masks_pe(12, 14, 4, 10)
+    complete_own(4)
+    let_mask(5)
+    complete_others(4, 0)
     text_list(2)
-    for d in range(4, 7):
-        fail_columns(d)
-        complete_own(d)
-        fail_gather(d + 1)
-        yg_ln(d - 1)
-        yg_round(d - 1)
-        text_gather(d - 1)
-        fail_ln(d + 1)
-        fail_list(d + 1)
-        if d == 4:
-            for i in range(8, 16):
-                text_mask(i, 4, 10)
-        text_ln(d - 1)
-        yg_out(d - 1)
-        if d == 6:
-            h = yf_numbers(0, 100, [H["mf5"]])
-            h = yf_turn("pm0", 0, 100, h)
-        complete_others(d)
-        if d == 6:
-            yf_out("pm0", "tr1", 0, 100, h)
-        text_list(d - 1)
-    wait("s", H["tab6"], H["fl7"])
-
-    def plain(q, r):
-        out = T.tab[:, BASE[7] + 512 * r:BASE[7] + 512 * r + 512]
-        src = T.tab[:, 0:BASE[7]].indirect(T.fl7[:, 32 * r:32 * r + 32])
-        if q == "s":
-            return fin("s", S.activation(out, src, F.Copy))
-        return fin("v", V.tensor_copy(out, src))
-
-    H["own7"] = plain("s", R)
-    text_gather(6)
-    yg_ln(6)
-    text_ln(6)
-    text_list(6)
+    text_gather(3)
+    fail_ln(5)
+    masks_out(m0)
+    fail_list(5)
+    masks_out(m1)
+    text_ln(3)
+    text_masks(14, 16, 4, 10)
+    complete_others(4, 1)
+    text_list(3)
+    H["nf2"] = fin("v", V.tensor_scalar(T.nf[:, 0:4], T.raw[:, slot + 68:slot + 72], 16.0, None, A.add))
+    yf_numbers(3)
+    fail_columns(5)
+    text_gather(4)
+    H["zz"] = fin("v", V.memset(T.zz[0:8, :], 0.0))
+    store(T.yf[:, 0:4], T.zz[0:8, :], H["zz"])
+    fail_gather(6)
+    complete_own(5)
+    running(("lnt", 1))
+    text_ln(4)
+    text_list(4)
+    running(("lnt", 2))
+    complete_others(5, 0)
+    yf_numbers(4)
+    running(("lnt", 3))
+    fail_ln(6)
+    fail_list(6)
+    running(("lnt", 4))
+    yf_numbers(5)
+    complete_others(5, 1)
+    yg_ln(2)
+    yg_round(2)
+    yg_out(2)
+    yg_ln(3)
+    yg_round(3)
+    H["onesf"] = fin("v", V.memset(T.onesf[:, :], 1.0))
+    wait("gc", H["onesf"])
+    H["ident"] = fin("gc", g.affine_select(T.ident[:, :], T.onesf[:, :], [[-1, 128]], A.is_equal, 0.0, 0, 1))
+    h = yf_turn("pm0", 0, 100, [H["nf%d" % d] for d in (2, 3, 4, 5)])
+    fail_columns(6)
+    H["tab6"] = [H["d6"]]
     rest = [r for r in range(4) if r != R]
-    wait("s", H["a_f7"])
-    wait("v", H["a_f7"])
-    H["tab7s"] = [H["own7"], plain("s", rest[0])]
-    plain("v", rest[1])
-    H["tab7"] = plain("v", rest[2])
+    text_gather(5)
+    fail_gather(7)
+    plain("s", rest[0])
+    plain("v", rest[2])
+    text_ln(5)
+    text_list(5)
+    plain("s", rest[1])
+    fail_ln(7)
+    deep_list(5)
+    text_gather(6)
+    fail_list(7)
+    deep_gather(6)
+    yf_out("pm0", "tr1", 0, 100, h)
+    wait("s", *H["tab6"])
+    wait("s", H["fl7"])
+    text_ln(6)
+    yf_numbers(6)
+    yf_numbers(7)
+    running(("lnt", 5))
+    H["h7"] = fin("s", S.activation(T.h7[:, :], T.tab[:, :].indirect(own_list(7)), F.Copy))
+    text_list(6)
     text_gather(7)
+    wait("v", H["fl6"], H["e6"], *H["tab5"])
+    H["own6"] = fin("v", V.tensor_tensor(T.g6[:, :], T.tab[:, 0:BASE[6]].indirect(own_list(6)), own_tc(6), A.max))
+    deep_list(6)
+    running(("lnt", 6))
+    yg_out(3)
+    deep_ln(6)
+    text_ln(7)
+    h7 = yf_turn("pm1", 100, 164, [H["nf6"], H["nf7"]])
+    yg_ln(6)
     yg_round(6)
     yg_out(6)
-    h7 = yf_numbers(100, 164, [H["mf6"], H["mf7"]])
-    text_ln(7)
+    running(("lnp", 6))
     text_list(7)
     text_gather(8)
-    h7 = yf_turn("pm1", 100, 164, h7)
-    yg_ln(7)
-    yf_out("pm1", "tr2", 100, 164, h7)
+    wait("v", H["h7"], H["flp"], H["a_t6"], H["fill"])
+    H["own7"] = fin("v", V.tensor_tensor(T.g7[:, :], T.tc6[:, :].indirect(T.flp[:, :]), T.h7[:, :], A.max))
+    deep_list(7)
+    running(("lnt", 7))
     text_ln(8)
+    yf_out("pm1", "tr2", 100, 164, h7)
+    yg_ln(4)
+    yg_round(4)
+    yg_out(4)
     text_list(8)
     text_gather(9)
-    yg_round(7)
-    yg_out(7)
+    deep_list(8)
+    deep_gather(9)
+    deep_gather(7)
+    running(("lnt", 8))
+    deep_gather(8)
     text_ln(9)
-    text_list(9)
-    store(T.yl[:, :], T.oyl[:, :], H["oyl"])
-    wait("v", H["rm9"])
-    h = fin("v", V.tensor_scalar(T.oym[:, :], T.rm[:, 288:320], 16.0 - MAGIC, None, A.add))
-    store(T.ym[:, :], T.oym[:, :], h)
+    yg_ln(7)
+    yg_round(7)
+    deep_ln(9)
+    yg_out(7)
+    deep_ln(7)
+    running(("lnp", 7))
+    deep_ln(8)
+    yg_ln(5)
+    yg_round(5)
+    yg_out(5)
+    running(("lnp", 8))
+    wait("v", H["lnt9"], H["lnp9"])
+    h = fin("v", V.tensor_tensor(T.last[:, 0:32], T.lnt[:, 288:320], T.lnp[:, 288:320], A.max))
+    wait("v", h, H["rm"])
+    h = fin("v", V.tensor_tensor(T.last[:, 32:64], T.rm[:, :], T.last[:, 0:32], A.max))
+    wait("v", h)
+    h = fin("v", V.tensor_scalar(T.lastm[:, :], T.last[:, :], 1.0 / K, float(MAGIC + A0), A.mult, A.add))
+    wait("v", h)
+    h = fin("v", V.tensor_scalar(T.oy[:, :], T.lastm[:, :], 16.0 - MAGIC, None, A.add))
+    store(T.yl[:, :], T.oy[:, 0:32], h)
+    store(T.ym[:, :], T.oy[:, 32:64], h)
     wait("gc", ("v", cnt["v"]), ("s", cnt["s"]), ("p", cnt["p"]), ("gc", cnt["gc"]), ("out", cnt["out"]), ("sent", cnt["sent"]))

from concourse.bass import DstId, RemoteDMATransfer
from concourse.mybir import AluOpType as A, ActivationFunctionType as F

K = 0.008435
A0 = 5256
NONE = 6e-20
MAGIC = 12582912
SIZE = {1: 4, 2: 64, 3: 512, 4: 512, 5: 512, 6: 512, 7: 512}
OWN = {1: 0, 2: 4, 3: 68, 4: 580, 5: 1092, 6: 1604, 7: 2116}
BASE = {1: 0, 2: 16, 3: 272, 4: 2320, 5: 4368, 6: 6416, 7: 8464}
SLOT = 72
PAD = {3: 0, 4: 0, 5: 0, 6: 16}

SCRATCH = {
    "tab": ("sbuf", [128, 8464], "bfloat16"), "raw": ("sbuf", [128, 4 * SLOT], "int32"),
    "c1f": ("sbuf", [128, 16], "float32"), "c2f": ("sbuf", [128, 256], "float32"), "c2": ("sbuf", [128, 256], "bfloat16"),
    "leti": ("sbuf", [128, 164], "int32"), "letb": ("sbuf", [128, 164], "bfloat16"), "maskl": ("sbuf", [128, 2624], "bfloat16"),
    "pari": ("sbuf", [128, 164], "int32"), "pu": ("sbuf", [128, 164], "uint16"),
    "vi": ("sbuf", [128, 320], "int32"), "vb": ("sbuf", [128, 320], "bfloat16"),
    "vq": ("sbuf", [128, 320], "bfloat16"), "maskt": ("sbuf", [128, 4608], "bfloat16"),
    "fl2": ("sbuf", [128, 16], "uint16"), "d2": ("sbuf", [128, 64], "bfloat16"),
    "lt": ("sbuf", [128, 320], "uint16"), "ltp": ("sbuf", [128, 320], "uint16"), "flp": ("sbuf", [128, 32], "uint16"),
    "lnf": ("sbuf", [128, 164], "float32"), "lnt": ("sbuf", [128, 320], "float32"), "lnp": ("sbuf", [128, 320], "float32"),
    "rm": ("sbuf", [128, 32], "float32"), "last": ("sbuf", [128, 64], "float32"), "lastm": ("sbuf", [128, 64], "float32"),
    "oy": ("sbuf", [128, 64], "float32"),
    "nf": ("sbuf", [128, 164], "float32"), "tr1": ("sbuf", [128, 128], "float32"), "tr2": ("sbuf", [128, 128], "float32"),
    "zz": ("sbuf", [128, 4], "float32"), "g6": ("sbuf", [128, 512], "bfloat16"),
    "h7": ("sbuf", [128, 512], "bfloat16"), "g7": ("sbuf", [128, 512], "bfloat16"),
    "ya": ("sbuf", [128, 2628], "float32"), "yb": ("sbuf", [128, 2628], "float32"), "yo": ("sbuf", [128, 2628], "float32"),
    "ones": ("sbuf", [128, 128], "bfloat16"), "blk0": ("sbuf", [128, 128], "bfloat16"), "blk": ("sbuf", [128, 128], "bfloat16"),
    "blk2": ("sbuf", [128, 128], "bfloat16"), "row2": ("sbuf", [128, 128], "bfloat16"),
    "onesf": ("sbuf", [128, 128], "float32"), "ident": ("sbuf", [128, 128], "float32"),
    "pcol": ("sbuf", [128, 1], "int32"), "cci": ("sbuf", [128, 1], "int32"), "ccf": ("sbuf", [128, 1], "float32"),
    "cc2": ("sbuf", [128, 1], "float32"), "bq": ("sbuf", [128, 1], "float32"),
    "row16": ("sbuf", [128, 16], "float32"), "ee": ("sbuf", [128, 16], "float32"),
    "brd": ("sbuf", [128, 2048], "bfloat16"), "br2": ("sbuf", [128, 2048], "bfloat16"), "sel": ("sbuf", [128, 2048], "bfloat16"),
}
for _d in range(3, 7):
    SCRATCH["ti%d" % _d] = ("sbuf", [128, 512], "int32")
    SCRATCH["cf%d" % _d] = ("sbuf", [128, 512], "float32")
    SCRATCH["tc%d" % _d] = ("sbuf", [128, PAD[_d] + 2048], "bfloat16")
for _d in range(3, 6):
    SCRATCH["d%d" % _d] = ("sbuf", [128, 512], "bfloat16")
for _d in range(3, 8):
    SCRATCH["fl%d" % _d] = ("sbuf", [128, 128], "uint16")
    SCRATCH["xf%d" % _d] = ("sbuf", [128, 512], "bfloat16")
for _t in range(1, 10):
    SCRATCH["xt%d" % _t] = ("sbuf", [128, 512], "bfloat16")
for _t in range(6, 10):
    SCRATCH["xp%d" % _t] = ("sbuf", [128, 512], "bfloat16")
for _b in ("pm0", "pm1", "pt0", "pt1", "pf0", "pf1", "px0", "px1"):
    SCRATCH[_b] = ("psum", [128, 512], "float32")

LOADS = ["ti12", "let", "ti3", "par", "txt", "ti4", "ti5", "ti6"]
SEMAPHORES = (["v", "s", "p", "gc", "out", "sent", "a_raw"] + ["ld_" + n for n in LOADS]
              + ["a_t%d" % d for d in range(3, 7)] + ["a_f%d" % d for d in range(3, 7)] + ["h%d" % d for d in range(4, 7)])


def helper_of(core, ranks, topo):
    for h in topo.cores_of(core):
        if h != core and topo.die(h) != topo.die(core) and all(topo.may_write(h, r) for r in ranks if r != core):
            return h
    return None


def bits(engines):
    m = 0
    for e in engines:
        m |= 1 << e
    return m


def dst_id(c, topo):
    rid, pid, _ = topo.addr(c)
    return DstId(rid=rid, pnc=pid)


def send(g, T, topo, core, dsts, ap, sem):
    g.remote_dma_fused([RemoteDMATransfer(dst_ids=[dst_id(c, topo) for c in dsts], dma_engine_mask=topo.mask(core, dsts[0]),
                                          remote_sem=T.sem[sem], srcs=[ap], dsts=[ap for c in dsts], alu_op=0)],
                       local_sem=T.sem["sent"])
    return len(topo.engines(core, dsts[0]))


def helper_program(g, core, T, topo, r):
    own = T.cores[r]
    others = [c for c in T.cores if c != own]
    near = spare_engines(own, core, others[0], topo)
    n = 0
    for d in range(4, 7):
        g.wait_ge(T.sem["h%d" % d], len(near))
        n += send(g, T, topo, core, others, T["tc%d" % d][:, PAD[d] + 512 * r:PAD[d] + 512 * r + 512], "a_t%d" % d)
    g.wait_ge(T.sem["sent"], n)


def spare_engines(core, helper, other, topo):
    far = set(topo.engines(core, other))
    return [e for e in topo.engines(core, helper) if e not in far]


def rank_program(g, core, T, topo):
    rank = T.rank_of(core)
    if rank is None:
        for i, c in enumerate(T.cores):
            if helper_of(c, T.cores, topo) == core:
                helper_program(g, core, T, topo, i)
        return
    R = rank
    others = [c for c in T.cores if c != core]
    helper = helper_of(core, T.cores, topo)
    queue = {"v": g.vector, "s": g.scalar, "p": g.tensor, "gc": g, "y": g.sync}
    cnt = {"v": 0, "s": 0, "p": 0, "gc": 0, "out": 0, "sent": 0}
    seen = {}

    def wait(q, *hs):
        for h in hs:
            if h is None:
                continue
            sem, val = h
            if seen.get((q, sem), 0) < val:
                queue[q].wait_ge(T.sem[sem], val)
                seen[(q, sem)] = val

    def fin(q, ins):
        cnt[q] += 1
        ins.then_inc(T.sem[q], 1)
        return (q, cnt[q])

    V, S, P = g.vector, g.scalar, g.tensor
    H = {}

    def load(name, pairs):
        for out, in_ in pairs:
            g.sync.dma_start(out, in_).then_inc(T.sem["ld_" + name], 16)
        H["ld_" + name] = ("ld_" + name, 16 * len(pairs))

    slot = SLOT * R
    load("ti12", [(T.raw[:, slot:slot + 68], T.tri[:, 0:68])]
         + [(T.raw[:, slot + 68 + j:slot + 69 + j], T.let[:, 16 * j:16 * j + 16]) for j in range(4)])
    load("ti3", [(T.ti3[:, :], T.tri[:, OWN[3]:OWN[4]])])
    load("let", [(T.leti[:, :], T.let[:, :])])
    load("par", [(T.pari[:, :], T.par[:, :])])
    for d in range(4, 7):
        load("ti%d" % d, [(T["ti%d" % d][:, :], T.tri[:, OWN[d]:OWN[d + 1]])])
    load("txt", [(T.vi[:, 32 * t:32 * t + 32], T.txt[:, 512 * t:512 * t + 512]) for t in range(10)])

    def store(out, in_, *hs):
        wait("y", *hs)
        g.sync.dma_start(out, in_).then_inc(T.sem["out"], 16)
        cnt["out"] += 16

    H["ones"] = fin("v", V.memset(T.ones[:, :], 1.0))
    H["pcol"] = fin("gc", g.iota(T.pcol[:, :], [[0, 1]], 0, 1))
    H["row16"] = fin("gc", g.iota(T.row16[:, :], [[1, 16]], 0, 0, allow_small_or_imprecise_dtypes=True))
    wait("gc", H["ones"])
    H["blk0"] = fin("gc", g.affine_select(T.blk0[:, :], T.ones[:, :], [[-16, 8], [0, 16]], A.is_ge, 0.0, 0, 1))
    wait("gc", H["blk0"])
    H["blk"] = fin("gc", g.affine_select(T.blk[:, :], T.blk0[:, :], [[16, 8], [0, 16]], A.is_ge, 0.0, 15, -1))
    H["row2"] = fin("gc", g.iota(T.row2[:, :], [[0, 8], [-2, 16]], 0, 0, allow_small_or_imprecise_dtypes=True))
    H["sel0"] = fin("v", V.memset(T.sel[:, :], 0.0))
    wait("v", H["pcol"])
    h = fin("v", V.tensor_scalar(T.cci[:, :], T.pcol[:, :], 15, None, A.bitwise_and))
    wait("v", h)
    H["ccf"] = fin("v", V.tensor_copy(T.ccf[:, :], T.cci[:, :]))
    wait("v", H["ccf"], H["row16"])
    H["ee"] = fin("v", V.tensor_scalar(T.ee[:, :], T.row16[:, :], T.ccf[:, 0:1], None, A.is_equal))
    h = fin("v", V.tensor_tensor(T.cc2[:, :], T.ccf[:, :], T.ccf[:, :], A.mult))
    wait("v", h, H["ee"], H["blk"])
    H["bq"] = fin("v", V.tensor_scalar(T.bq[:, :], T.cc2[:, :], -1.0, 1.0, A.mult, A.add))
    wait("s", H["sel0"], H["blk"])
    for i in range(16):
        H["sel"] = fin("s", S.activation(T.sel[:, 129 * i:128 * (i + 1):16], T.blk[:, i:128:16], F.Copy))
    for i in range(16):
        H["brd"] = fin("v", V.tensor_scalar(T.brd[:, 128 * i:128 * i + 128], T.blk[:, :], T.ee[:, i:i + 1], None, A.mult))
    wait("v", H["row2"])
    h2 = fin("v", V.tensor_tensor(T.blk2[:, :], T.blk[:, :], T.row2[:, :], A.mult))
    H["fill"] = fin("v", V.memset(T.tc6[:, 0:PAD[6]], NONE))
    wait("v", h2)
    for i in range(16):
        H["br2"] = fin("v", V.tensor_scalar(T.br2[:, 128 * i:128 * i + 128], T.blk2[:, :], T.ee[:, i:i + 1], None, A.mult))

    def code(out, in_, *hs):
        wait("s", *hs)
        return fin("s", S.activation(out, in_, F.Exp, bias=-K * (16 + A0), scale=K))

    def out_to_ranks(ap, sem, *hs):
        wait("gc", *hs)
        cnt["sent"] += send(g, T, topo, core, others, ap, sem)
        H[sem] = (sem, len(others) * len(topo.engines(core, others[0])))

    def own_tc(d):
        return T["tc%d" % d][:, PAD[d] + 512 * R:PAD[d] + 512 * R + 512]

    def pointers(d):
        wait("v", H["ld_ti%d" % d])
        h = fin("v", V.tensor_copy(T["cf%d" % d][:, :], T["ti%d" % d][:, :]))
        H["e%d" % d] = code(own_tc(d), T["cf%d" % d][:, :], h)

    def to_helper(d):
        eng = spare_engines(core, helper, others[0], topo)
        wait("gc", H["e%d" % d])
        rid, pid, _ = topo.addr(helper)
        g.remote_dma(own_tc(d), own_tc(d), T.sem["h%d" % d], T.sem["sent"], pid, rid, bits(eng))
        cnt["sent"] += len(eng)
        H["a_t%d" % d] = ("a_t%d" % d, len(others) * len(topo.engines(helper, others[0])))

    out_to_ranks(T.raw[:, slot:slot + SLOT], "a_raw", H["ld_ti12"])
    pointers(3)
    out_to_ranks(own_tc(3), "a_t3", H["e3"])

    last = {}

    wait("v", H["ld_let"])
    H["letb"] = fin("v", V.tensor_copy(T.letb[:, :], T.leti[:, :]))
    wait("v", H["ld_par"])
    H["pu"] = fin("v", V.tensor_copy(T.pu[:, :], T.pari[:, :]))
    LB = ["pm0", "pm1", "px0", "px1", "pm0", "pm1"]

    def let_pe(k):
        b = LB[k]
        wait("p", H["brd"], H["letb"], last.get(b))
        for n, i in enumerate(range(3 * k, min(3 * k + 3, 16))):
            H["letp%d" % k] = fin("p", P.matmul(T[b][:, 164 * n:164 * n + 164], T.brd[:, 128 * i:128 * i + 128], T.letb[:, :], True, True))

    def let_mask(k):
        b = LB[k]
        n = 164 * (min(3 * k + 3, 16) - 3 * k)
        wait("v", H["letp%d" % k], H["ccf"])
        last[b] = H["ml%d" % k] = fin("v", V.tensor_scalar(T.maskl[:, 492 * k:492 * k + n], T[b][:, 0:n], T.ccf[:, 0:1], None, A.is_equal))

    def let_seg(d):
        lo, hi = OWN[d] - 4, OWN[d] - 4 + 512
        return [H["ml%d" % k] for k in range(6) if 492 * k < hi and 492 * (k + 1) > lo]

    tn = [0]

    def masks_pe(lo, hi, t0, t1):
        b = "pt%d" % (tn[0] % 2)
        tn[0] += 1
        n = 32 * (t1 - t0)
        wait("p", H["br2"], H["brd"], H["vb"], H["vq"], last.get(b))
        for m, i in enumerate(range(lo, hi)):
            ap = T[b][:, m * n:m * n + n]
            P.matmul(ap, T.br2[:, 128 * i:128 * i + 128], T.vb[:, 32 * t0:32 * t1], True, False).then_inc(T.sem["p"], 1)
            cnt["p"] += 1
            h = fin("p", P.matmul(ap, T.brd[:, 128 * i:128 * i + 128], T.vq[:, 32 * t0:32 * t1], False, True))
        return (b, h, lo, hi, t0, n)

    def masks_out(made):
        b, h, lo, hi, t0, n = made
        wait("s", h, H["bq"])
        o = 512 * (t0 - 1)
        for m, i in enumerate(range(lo, hi)):
            last[b] = H["mt%d" % t0] = fin("s", S.activation(T.maskt[:, o + i:o + 16 * n:16], T[b][:, m * n:m * n + n], F.Relu,
                                                             bias=T.bq[:, 0:1], scale=-1.0))

    def text_masks(*which):
        masks_out(masks_pe(*which))

    let_pe(0)
    let_pe(1)
    let_pe(2)
    let_pe(3)
    pointers(4)
    to_helper(4)
    let_mask(0)
    let_mask(1)
    pointers(5)
    to_helper(5)
    pointers(6)
    to_helper(6)

    def sums(bank, x, hx):
        wait("p", hx, H["sel"], last.get(bank))
        for i in range(16):
            h = fin("p", P.matmul(T[bank][:, 0:32], T.sel[:, 128 * i:128 * i + 128], T[x][:, i:512:16], i == 0, i == 15))
        return h

    def fail_cols(d):
        if d == 6:
            return T.tab[:, BASE[6] + 512 * R:BASE[6] + 512 * R + 512]
        return T["d%d" % d][:, :]

    def fail_gather(d):
        q = OWN[d] - 4
        wait("v", H["d%d" % (d - 1)], H["pu"], *let_seg(d))
        h = fin("v", V.tensor_tensor(T["xf%d" % d][:, :], fail_cols(d - 1).indirect(T.pu[:, q // 16:q // 16 + 32]),
                                     T.maskl[:, q:q + 512], A.mult))
        H["xf%d" % d] = sums("pf%d" % (d % 2), "xf%d" % d, h)

    def fail_ln(d):
        j = (OWN[d] - 4) // 16
        wait("s", H["xf%d" % d])
        last["pf%d" % (d % 2)] = H["lnf%d" % d] = fin("s", S.activation(T.lnf[:, j:j + 32], T["pf%d" % (d % 2)][:, 0:32], F.Ln))

    def own_list(d):
        return T["fl%d" % d][:, 32 * R:32 * R + 32]

    def fail_list(d):
        j = (OWN[d] - 4) // 16
        wait("v", H["lnf%d" % d])
        H["fl%d" % d] = fin("v", V.tensor_scalar(own_list(d), T.lnf[:, j:j + 32], 1.0 / K, float(A0), A.mult, A.add))
        if d < 7:
            out_to_ranks(own_list(d), "a_f%d" % d, H["fl%d" % d])
        else:
            H["flp"] = fin("v", V.tensor_scalar(T.flp[:, :], T.lnf[:, j:j + 32], 1.0 / K, float(A0 - BASE[6] + PAD[6]), A.mult, A.add))

    def text_gather(t):
        d = min(t, 6)
        wait("v", H["lt%d" % (t - 1)], H["mt1" if t < 4 else "mt4"], *H["tab%d" % d])
        h = fin("v", V.tensor_tensor(T["xt%d" % t][:, :], T.tab[:, 0:BASE[d + 1]].indirect(T.lt[:, 32 * t - 32:32 * t]),
                                     T.maskt[:, 512 * t - 512:512 * t], A.mult))
        H["xt%d" % t] = sums("px%d" % (t % 2), "xt%d" % t, h)

    def text_ln(t):
        wait("s", H["xt%d" % t])
        last["px%d" % (t % 2)] = H["lnt%d" % t] = fin("s", S.activation(T.lnt[:, 32 * t:32 * t + 32], T["px%d" % (t % 2)][:, 0:32], F.Ln))

    def text_list(t):
        c = slice(32 * t, 32 * t + 32)
        wait("v", H["lnt%d" % t])
        H["lt%d" % t] = fin("v", V.tensor_scalar(T.lt[:, c], T.lnt[:, c], 1.0 / K, float(A0), A.mult, A.add))

    def deep_list(t):
        c = slice(32 * t, 32 * t + 32)
        wait("v", H["lnt%d" % t])
        H["ltp%d" % t] = fin("v", V.tensor_scalar(T.ltp[:, c], T.lnt[:, c], 1.0 / K, float(A0 - BASE[6] + PAD[6]), A.mult, A.add))

    DB = {6: "pt0", 7: "pt1", 8: "pf0", 9: "pf1"}

    def deep_gather(t):
        wait("v", H["ltp%d" % (t - 1)], H["a_t6"], H["e6"], H["fill"])
        h = fin("v", V.tensor_tensor(T["xp%d" % t][:, :], T.tc6[:, :].indirect(T.ltp[:, 32 * t - 32:32 * t]),
                                     T.maskt[:, 512 * t - 512:512 * t], A.mult))
        H["xp%d" % t] = sums(DB[t], "xp%d" % t, h)

    def deep_ln(t):
        wait("s", H["xp%d" % t])
        last[DB[t]] = H["lnp%d" % t] = fin("s", S.activation(T.lnp[:, 32 * t:32 * t + 32], T[DB[t]][:, 0:32], F.Ln))

    def running(*names):
        for buf, t in names:
            ap = T[buf][:, 32 * t:32 * t + 32]
            wait("v", H["%s%d" % (buf, t)], H.get("rm"))
            if "rm" in H:
                H["rm"] = fin("v", V.tensor_tensor(T.rm[:, :], T.rm[:, :], ap, A.max))
            else:
                H["rm"] = fin("v", V.tensor_copy(T.rm[:, :], ap))

    def fail_columns(d):
        wait("s", *H["tab%d" % (d - 1)])
        wait("s", H["fl%d" % d])
        off = T.fl2[:, 4 * R:4 * R + 4] if d == 2 else own_list(d)
        out = T.d2[:, :] if d == 2 else fail_cols(d)
        H["d%d" % d] = fin("s", S.activation(out, T.tab[:, 0:BASE[d]].indirect(off), F.Copy))

    def complete(d, c0, c1):
        if c0 < c1:
            wait("v", *H["tab%d" % (d - 1)])
            return [fin("v", V.tensor_tensor(T.tab[:, BASE[d] + 16 * c0:BASE[d] + 16 * c1],
                                             T.tab[:, 0:BASE[d]].indirect(T["fl%d" % d][:, c0:c1]),
                                             T["tc%d" % d][:, 16 * c0:16 * c1], A.max))]
        return []

    def complete_own(d):
        wait("v", H["fl%d" % d], H["e%d" % d])
        H["tab%d" % d] = complete(d, 32 * R, 32 * R + 32)
        H["own%d" % d] = H["tab%d" % d][0]

    def complete_others(d, part):
        wait("v", H["a_f%d" % d], H["a_t%d" % d])
        cuts = [(0, 16), (16, 32 * R), (32 * R + 32, 128)] if R else [(32, 48), (48, 128)]
        for c in (cuts[:1] if part == 0 else cuts[1:]):
            H["tab%d" % d] += complete(d, *c)

    def plain(q, r):
        off = T.fl6[:, 32 * r:32 * r + 32]
        out = T.tab[:, BASE[6] + 512 * r:BASE[6] + 512 * r + 512]
        src = T.tab[:, 0:BASE[6]].indirect(off)
        wait(q, *H["tab5"])
        wait(q, H["a_f6"])
        if q == "s":
            h = fin("s", S.activation(out, src, F.Copy))
        else:
            h = fin("v", V.tensor_copy(out, src))
        H["tab6"].append(h)

    def own_ap(d):
        if d >= 6:
            return T["g%d" % d][:, :]
        return T.tab[:, BASE[d] + SIZE[d] * R:BASE[d] + SIZE[d] * R + SIZE[d]]

    def yg_ln(d):
        c = slice(OWN[d], OWN[d] + SIZE[d])
        wait("s", H["own%d" % d])
        H["ya%d" % d] = fin("s", S.activation(T.ya[:, c], own_ap(d), F.Ln))

    def yg_cols(d):
        return slice(0 if d == 2 else OWN[d], OWN[d] + SIZE[d])

    def yg_round(d):
        wait("s", H["ya%d" % d])
        H["yb%d" % d] = fin("s", S.activation(T.yb[:, yg_cols(d)], T.ya[:, yg_cols(d)], F.Identity, bias=float(MAGIC + A0), scale=1.0 / K))

    def yg_out(d):
        wait("s", H["yb%d" % d])
        h = fin("s", S.activation(T.yo[:, yg_cols(d)], T.yb[:, yg_cols(d)], F.Identity, bias=16.0 - MAGIC))
        store(T.yg[:, yg_cols(d)], T.yo[:, yg_cols(d)], h)

    def yf_numbers(d):
        j = (OWN[d] - 4) // 16
        wait("v", H["fl%d" % d])
        H["nf%d" % d] = fin("v", V.tensor_scalar(T.nf[:, j:j + 32], own_list(d), 16.0, None, A.add))

    def yf_turn(bank, j0, j1, hs):
        wait("p", *hs)
        wait("p", H["ident"], last.get(bank))
        return fin("p", P.transpose(T[bank][0:j1 - j0, 0:128], T.nf[:, j0:j1], T.ident[:, :]))

    def yf_out(bank, buf, j0, j1, h):
        n = j1 - j0
        wait("s", h)
        h = fin("s", S.activation(T[buf][0:n, :], T[bank][0:n, 0:128], F.Copy))
        for k in range(8):
            store(T.yf[k:k + 1, 4 + 16 * j0:4 + 16 * j1], T[buf][0:n, 16 * k:16 * k + 16], h)

    wait("v", H["a_raw"], H["ld_ti12"])
    for r in range(4):
        h = fin("v", V.tensor_copy(T.c1f[:, 4 * r:4 * r + 4], T.raw[:, SLOT * r:SLOT * r + 4]))
    H["tab1"] = [code(T.tab[:, 0:16], T.c1f[:, :], h)]
    for r in range(4):
        H["fl2"] = fin("v", V.tensor_copy(T.fl2[:, 4 * r:4 * r + 4], T.raw[:, SLOT * r + 68:SLOT * r + 72]))
    fail_columns(2)
    for r in range(4):
        h = fin("v", V.tensor_copy(T.c2f[:, 64 * r:64 * r + 64], T.raw[:, SLOT * r + 4:SLOT * r + 68]))
    H["c2"] = code(T.c2[:, :], T.c2f[:, :], h)
    H["own1"] = H["tab1"][0]
    yg_ln(1)
    fail_gather(3)
    wait("v", H["ld_txt"])
    H["vb"] = fin("v", V.tensor_copy(T.vb[:, :], T.vi[:, :]))
    wait("s", H["vb"])
    H["vq"] = fin("s", S.activation(T.vq[:, :], T.vb[:, :], F.Square))
    wait("v", H["c2"], *H["tab1"])
    H["own2"] = fin("v", V.tensor_tensor(T.tab[:, 16:272], T.tab[:, 0:16].indirect(T.fl2[:, :]), T.c2[:, :], A.max))
    H["tab2"] = [H["own2"]]
    H["lt0"] = fin("v", V.tensor_copy(T.lt[:, 0:32], T.vi[:, 0:32]))
    fail_ln(3)
    fail_list(3)
    fail_columns(3)
    text_masks(0, 5, 1, 4)
    text_masks(5, 10, 1, 4)
    text_masks(10, 15, 1, 4)
    text_masks(15, 16, 1, 4)
    complete_own(3)
    let_mask(2)
    fail_gather(4)
    let_mask(3)
    let_pe(4)
    let_pe(5)
    m0 = masks_pe(0, 2, 4, 10)
    m1 = masks_pe(2, 4, 4, 10)
    complete_others(3, 0)
    text_gather(1)
    fail_ln(4)
    fail_list(4)
    masks_out(m0)
    masks_out(m1)
    text_ln(1)
    complete_others(3, 1)
    text_list(1)
    fail_columns(4)
    text_masks(4, 6, 4, 10)
    text_masks(6, 8, 4, 10)
    text_gather(2)
    let_mask(4)
    fail_gather(5)
    text_ln(2)
    text_masks(8, 10, 4, 10)
    m0 = masks_pe(10, 12, 4, 10)
    m1 = masks_pe(12, 14, 4, 10)
    complete_own(4)
    let_mask(5)
    complete_others(4, 0)
    text_list(2)
    text_gather(3)
    fail_ln(5)
    masks_out(m0)
    fail_list(5)
    masks_out(m1)
    text_ln(3)
    text_masks(14, 16, 4, 10)
    complete_others(4, 1)
    text_list(3)
    H["nf2"] = fin("v", V.tensor_scalar(T.nf[:, 0:4], T.raw[:, slot + 68:slot + 72], 16.0, None, A.add))
    yf_numbers(3)
    fail_columns(5)
    text_gather(4)
    H["zz"] = fin("v", V.memset(T.zz[0:8, :], 0.0))
    store(T.yf[:, 0:4], T.zz[0:8, :], H["zz"])
    fail_gather(6)
    complete_own(5)
    running(("lnt", 1))
    text_ln(4)
    text_list(4)
    running(("lnt", 2))
    complete_others(5, 0)
    yf_numbers(4)
    running(("lnt", 3))
    fail_ln(6)
    fail_list(6)
    running(("lnt", 4))
    yf_numbers(5)
    complete_others(5, 1)
    yg_ln(2)
    yg_round(2)
    yg_out(2)
    yg_ln(3)
    yg_round(3)
    H["onesf"] = fin("v", V.memset(T.onesf[:, :], 1.0))
    wait("gc", H["onesf"])
    H["ident"] = fin("gc", g.affine_select(T.ident[:, :], T.onesf[:, :], [[-1, 128]], A.is_equal, 0.0, 0, 1))
    h = yf_turn("pm0", 0, 100, [H["nf%d" % d] for d in (2, 3, 4, 5)])
    fail_columns(6)
    H["tab6"] = [H["d6"]]
    rest = [r for r in range(4) if r != R]
    text_gather(5)
    fail_gather(7)
    plain("s", rest[0])
    plain("v", rest[2])
    text_ln(5)
    text_list(5)
    plain("s", rest[1])
    fail_ln(7)
    deep_list(5)
    text_gather(6)
    fail_list(7)
    deep_gather(6)
    yf_out("pm0", "tr1", 0, 100, h)
    wait("s", *H["tab6"])
    wait("s", H["fl7"])
    text_ln(6)
    yf_numbers(6)
    yf_numbers(7)
    running(("lnt", 5))
    H["h7"] = fin("s", S.activation(T.h7[:, :], T.tab[:, :].indirect(own_list(7)), F.Copy))
    text_list(6)
    text_gather(7)
    wait("v", H["fl6"], H["e6"], *H["tab5"])
    H["own6"] = fin("v", V.tensor_tensor(T.g6[:, :], T.tab[:, 0:BASE[6]].indirect(own_list(6)), own_tc(6), A.max))
    deep_list(6)
    running(("lnt", 6))
    yg_out(3)
    deep_ln(6)
    text_ln(7)
    h7 = yf_turn("pm1", 100, 164, [H["nf6"], H["nf7"]])
    yg_ln(6)
    yg_round(6)
    yg_out(6)
    running(("lnp", 6))
    text_list(7)
    text_gather(8)
    wait("v", H["h7"], H["flp"], H["a_t6"], H["fill"])
    H["own7"] = fin("v", V.tensor_tensor(T.g7[:, :], T.tc6[:, :].indirect(T.flp[:, :]), T.h7[:, :], A.max))
    deep_list(7)
    running(("lnt", 7))
    text_ln(8)
    yf_out("pm1", "tr2", 100, 164, h7)
    yg_ln(4)
    yg_round(4)
    yg_out(4)
    text_list(8)
    text_gather(9)
    deep_list(8)
    deep_gather(9)
    deep_gather(7)
    running(("lnt", 8))
    deep_gather(8)
    text_ln(9)
    yg_ln(7)
    yg_round(7)
    deep_ln(9)
    yg_out(7)
    deep_ln(7)
    running(("lnp", 7))
    deep_ln(8)
    yg_ln(5)
    yg_round(5)
    yg_out(5)
    running(("lnp", 8))
    wait("v", H["lnt9"], H["lnp9"])
    h = fin("v", V.tensor_tensor(T.last[:, 0:32], T.lnt[:, 288:320], T.lnp[:, 288:320], A.max))
    wait("v", h, H["rm"])
    h = fin("v", V.tensor_tensor(T.last[:, 32:64], T.rm[:, :], T.last[:, 0:32], A.max))
    wait("v", h)
    h = fin("v", V.tensor_scalar(T.lastm[:, :], T.last[:, :], 1.0 / K, float(MAGIC + A0), A.mult, A.add))
    wait("v", h)
    h = fin("v", V.tensor_scalar(T.oy[:, :], T.lastm[:, :], 16.0 - MAGIC, None, A.add))
    store(T.yl[:, :], T.oy[:, 0:32], h)
    store(T.ym[:, :], T.oy[:, 32:64], h)
    wait("gc", ("v", cnt["v"]), ("s", cnt["s"]), ("p", cnt["p"]), ("gc", cnt["gc"]), ("out", cnt["out"]), ("sent", cnt["sent"]))
